import numpy as np
import ml_dtypes


def mxq(x, axis, fmt="e4m3"):
    dtype, down = {"e4m3": (ml_dtypes.float8_e4m3fn, 7), "e5m2": (ml_dtypes.float8_e5m2, 14)}[fmt]
    v = np.moveaxis(np.asarray(x, np.float32).astype(ml_dtypes.bfloat16).astype(np.float64), axis, -1)
    blocks = v.reshape(v.shape[:-1] + (-1, 32))
    amax = np.abs(blocks).max(-1, keepdims=True)
    byte = np.maximum(np.where(amax > 0, np.frexp(amax)[1] - 1 + 127, 0) - down, 1)
    scale = np.exp2(byte - 127.0)
    codes = (blocks / scale).astype(np.float32).astype(dtype).astype(np.float64)
    return np.moveaxis((codes * scale).reshape(v.shape), -1, axis)


WIDE = False


def mx_kscale(k):
    if not WIDE:
        return np.ones(k)
    levels = np.array([10, -10, 5, -5, 0])
    if k % 512:
        return np.exp2(np.random.permutation(np.resize(levels, k // 32))).repeat(32)
    a = np.empty((k // 512, 16))
    for p in range(k // 512):
        a[p, :8] = np.random.permutation(np.resize(levels, 8))
        for g in range(8):
            far = levels[np.abs(levels - a[p, g]) >= 10]
            a[p, g + 8] = far[np.random.randint(len(far))]
    return np.exp2(a.ravel()).repeat(32)


def f64(x):
    return np.asarray(x).astype(np.float64)


def striped(idx):
    return np.tile(idx.reshape(-1, 16).T, (8, 1)).astype(np.uint16)


def unstriped(offs):
    return offs[:16].T.reshape(-1).astype(np.int64)


E2M1 = np.array([0.0, 0.5, 1.0, 1.5, 2.0, 3.0, 4.0, 6.0, -0.0, -0.5, -1.0, -1.5, -2.0, -3.0, -4.0, -6.0])


def pack_weight(w, fmt):
    k, n = w.shape
    w = f64(np.asarray(w, np.float32).astype(ml_dtypes.bfloat16)).reshape(k // 32, 32, n)
    amax = np.abs(w).max(1)
    if fmt == "e4m3":
        byte = np.frexp(amax)[1] - 1 + 127 - 7
    else:
        mant, ex = np.frexp(amax / 6.0)
        byte = np.where(mant > 0.5, ex, ex - 1) + 127
    byte = np.clip(np.where(amax > 0, byte, 1), 1, 254)
    scaled = (w * np.exp2(127.0 - byte)[:, None, :]).reshape(k, n).astype(np.float32)
    by_word = np.ascontiguousarray(scaled.reshape(k // 512, 128, 4, n).transpose(0, 1, 3, 2))
    if fmt == "e4m3":
        words = by_word.astype(ml_dtypes.float8_e4m3fn).view(np.uint8)
    else:
        c = by_word.astype(ml_dtypes.float4_e2m1fn).view(np.uint8) & 0xF
        words = (c[..., 0::2] | (c[..., 1::2] << 4)).reshape(k // 512, 128, 2 * n)
    return np.ascontiguousarray(words), np.ascontiguousarray(byte.astype(np.uint8).reshape(k // 512, 16, n))


def unpack_weight(words, scales, fmt):
    g, _, n = scales.shape
    words = np.ascontiguousarray(words).reshape(g, 128, n, -1)
    if fmt == "e4m3":
        vals = words.view(ml_dtypes.float8_e4m3fn).astype(np.float64)
    else:
        nib = np.empty((g, 128, n, 4), np.uint8)
        nib[..., 0::2] = words & 0xF
        nib[..., 1::2] = words >> 4
        vals = E2M1[nib]
    vals = vals * np.repeat(np.exp2(scales.astype(np.float64) - 127.0), 8, axis=1)[..., None]
    return vals.transpose(0, 1, 3, 2).reshape(g * 512, n)


def gelu(v):
    return 0.5 * v * (1.0 + np.tanh(np.sqrt(2.0 / np.pi) * (v + 0.044715 * v**3)))


K, T, S, H, N, LANES = 1024, 4096, 1024, 1024, 512, 128

def setup_inputs():
    n = np.random.standard_normal
    s = mx_kscale(K)[:, None]
    u = mx_kscale(H)[:, None]
    tab_words, tab_scales = pack_weight(n((K, T)) * s, "e4m3")
    w4_words, w4_scales = pack_weight(n((K, H)) * 0.5 / np.sqrt(K) / s, "e2m1")
    wb = (n((K, H)) * 0.5 / np.sqrt(K) / s).astype(np.float32)
    w8_words, w8_scales = pack_weight(n((H, N)) / np.sqrt(H) / u, "e4m3")
    return {
        "tab_words": tab_words, "tab_scales": tab_scales,
        "offs": striped(np.random.permutation(T)[:S]),
        "w4_words": w4_words, "w4_scales": w4_scales,
        "wb": wb,
        "gain": (np.exp(0.3 * n(H)) * u[:, 0]).astype(np.float32),
        "w8_words": w8_words, "w8_scales": w8_scales,
        "offs2": striped(np.random.permutation(S)),
        "wgo": np.exp(0.3 * n((LANES, S))).astype(np.float32),
        "x0": n((N, S)).astype(np.float32),
    }

def reference(tab_words, tab_scales, offs, w4_words, w4_scales, wb, gain,
              w8_words, w8_scales, offs2, wgo, x0):
    v = unpack_weight(tab_words, tab_scales, "e4m3")[:, unstriped(offs)]
    a = unpack_weight(w4_words, w4_scales, "e2m1").T @ v
    b = mxq(f64(wb), 0, "e4m3").T @ v
    h = f64(gain)[:, None] * (np.exp(a) - np.exp(b))
    y = unpack_weight(w8_words, w8_scales, "e4m3").T @ mxq(h, 0, "e4m3")
    page = np.zeros((N, S))
    page[:, unstriped(offs2)] = np.tile(f64(wgo), (N // LANES, 1)) * y
    return np.abs(f64(x0) - page)

@@ -1,0 +1,321 @@
+from contextlib import ExitStack
+
+import concourse.mybir as mybir
+from concourse.masks import make_identity
+
+K, T, S, H, N = 1024, 4096, 1024, 1024, 512
+FLOPS = 2 * (2 * K * H * S + H * N * S)
+
+F32 = mybir.dt.float32
+BF16 = mybir.dt.bfloat16
+I32 = mybir.dt.int32
+U32 = mybir.dt.uint32
+U16 = mybir.dt.uint16
+U8 = mybir.dt.uint8
+E4M3 = mybir.dt.float8_e4m3fn_x4
+E2M1 = mybir.dt.float4_e2m1fn_x4
+ALU = mybir.AluOpType
+ACT = mybir.ActivationFunctionType
+
+P = 128
+PACK = 4
+PASS = P * PACK
+QUADS = 4
+HALF = 512
+PIECE = 256
+LIST = 16
+
+V_AT, W4_AT, W8_AT, ROW = 0, S, S + H, S + H + N
+
+TINY, LIFT = 2.0**-50, 2.0**90
+HUGE, DROP = 2.0**50, 2.0**-70
+FLOOR = 2.0**-60
+
+
+def tile_list_elution_balance_gap_kernel(
+    tc, tab_words, tab_scales, offs, w4_words, w4_scales, wb, gain, w8_words, w8_scales, offs2, wgo, x0, out
+):
+    nc = tc.nc
+    with ExitStack() as ctx:
+        lists = ctx.enter_context(tc.tile_pool(name="lists", bufs=1))
+        keep = ctx.enter_context(tc.tile_pool(name="keep", bufs=1))
+        big = ctx.enter_context(tc.tile_pool(name="big", bufs=2))
+        ring = ctx.enter_context(tc.tile_pool(name="ring", bufs=2))
+        ybuf = ctx.enter_context(tc.tile_pool(name="ybuf", bufs=7))
+        ab_psum = ctx.enter_context(tc.psum_pool(name="ab_psum", bufs=6))
+        y_psum = ctx.enter_context(tc.psum_pool(name="y_psum", bufs=2))
+
+        pick = lists.tile([P, S // LIST], U16, name="pick")
+        place = lists.tile([P, S // LIST], U16, name="place")
+
+        tab_rows = keep.tile([P, T], U8, name="tab_rows", align_bytes=64)
+        w4_rows = keep.tile([P, H], U8, name="w4_rows", align_bytes=64)
+        rows = keep.tile([P, ROW], U8, name="rows", align_bytes=64)
+        planes = keep.tile([P, 2 * ROW], U8, name="planes", align_bytes=64)
+        for loaded in (tab_rows, w4_rows):
+            nc.vector.memset(loaded[:].bitcast(I32)[32:64, :], 0)
+            nc.vector.memset(loaded[:].bitcast(I32)[64:128, :], 0)
+        nc.gpsimd.memset(planes[:].bitcast(I32), 0)
+
+        def plane(a, first, width):
+            return planes[:, a * ROW + first : a * ROW + first + width]
+
+        nc.sync.dma_start(tab_rows[:].bitcast(I32)[0:32, :], tab_scales.rearrange("a q t -> (a q) t").bitcast(I32))
+        nc.sync.dma_start(pick[:], offs)
+        nc.sync.dma_start(w4_rows[:].bitcast(I32)[0:32, :], w4_scales.rearrange("a q c -> (a q) c").bitcast(I32))
+        nc.sync.dma_start(
+            rows[:, W8_AT:].bitcast(I32)[0:32, :], w8_scales.rearrange("b q n -> (b q) n").bitcast(I32)
+        )
+        gain_sb = keep.tile([P, 2 * PACK], F32, name="gain_sb")
+        nc.sync.dma_start(
+            gain_sb[:].rearrange("p (b t) -> p b t", t=PACK), gain.rearrange("(b p t) -> p b t", p=P, t=PACK)
+        )
+        tab = []
+        for a in range(2):
+            tab.append(big.tile([P, T], I32, name="tab%d" % a, tag="wide", align_bytes=64))
+        nc.sync.dma_start(tab[0][:], tab_words[0].rearrange("p t i -> p (t i)").bitcast(I32))
+        w4_raw = keep.tile([P, 4 * H], U8, name="w4_raw", align_bytes=64)
+        nc.sync.dma_start(
+            w4_raw[:].bitcast(I32).rearrange("p (a c) -> p a c", a=2), w4_words.bitcast(I32).rearrange("a p c -> p a c")
+        )
+        nc.sync.dma_start(tab[1][:], tab_words[1].rearrange("p t i -> p (t i)").bitcast(I32))
+        wb_raw = {}
+        for b in range(2):
+            for a in range(2):
+                wb_raw[a, b] = keep.tile([P, PACK, PASS], F32, name="wb_raw%d%d" % (a, b))
+                nc.sync.dma_start(
+                    wb_raw[a, b][:],
+                    wb[a * PASS : (a + 1) * PASS, b * PASS : (b + 1) * PASS].rearrange("(p i) c -> p i c", i=PACK),
+                )
+        w8 = keep.tile([P, 2, N], I32, name="w8", align_bytes=64)
+        nc.sync.dma_start(w8[:], w8_words.rearrange("b p n i -> p b (n i)").bitcast(I32))
+        nc.sync.dma_start(place[:], offs2)
+        wgo_sb = keep.tile([P, S], F32, name="wgo_sb")
+        nc.sync.dma_start(wgo_sb[:], wgo)
+        gap = big.tile([P, N // P, S], F32, name="gap", tag="wide", align_bytes=64)
+        for n in range(N // P):
+            nc.sync.dma_start(gap[:, n, :], x0[n * P : (n + 1) * P, :])
+
+        v_rows = keep.tile([P, S], U8, name="v_rows", align_bytes=64)
+        nc.vector.tensor_copy(v_rows[:], tab_rows[:].indirect(pick[:]))
+        nc.vector.tensor_copy(
+            rows[:, W4_AT:W8_AT].rearrange("p (b t m e) -> p b m t e", b=2, t=PACK, e=16),
+            w4_rows[:].rearrange("p (b m e t) -> p b m t e", b=2, t=PACK, e=16),
+        )
+        nc.vector.tensor_copy(rows[:, V_AT:W4_AT].bitcast(I32), v_rows[:].bitcast(I32))
+        for a in range(2):
+            for q in range(QUADS):
+                row = 16 * a + 4 * q
+                nc.gpsimd.dma_start(
+                    plane(a, 0, ROW).bitcast(I32)[32 * q : 32 * q + 4, :], rows[:].bitcast(I32)[row : row + 4, :]
+                )
+        def column(name):
+            return keep.tile([P, 2 * PACK], F32, name=name)
+
+        size, small, large, mid = column("size"), column("small"), column("large"), column("mid")
+        shift, unshift, sign, inner = column("shift"), column("unshift"), column("sign"), column("inner")
+        log0, back, log_gain = column("log0"), column("back"), column("log_gain")
+        nc.vector.scalar_tensor_tensor(size[:], gain_sb[:], -1.0, gain_sb[:], ALU.mult, ALU.max)
+        nc.vector.tensor_scalar(small[:], size[:], TINY, None, ALU.is_lt)
+        nc.vector.tensor_scalar(large[:], size[:], HUGE, None, ALU.is_gt)
+        nc.vector.tensor_scalar(sign[:], gain_sb[:], 0.0, None, ALU.is_lt)
+        nc.vector.scalar_tensor_tensor(mid[:], small[:], -1.0, large[:], ALU.mult, ALU.subtract)
+        nc.vector.scalar_tensor_tensor(sign[:], gain_sb[:], 0.0, sign[:], ALU.is_gt, ALU.subtract)
+        nc.vector.tensor_scalar(mid[:], mid[:], 1.0, None, ALU.add)
+        nc.vector.scalar_tensor_tensor(shift[:], small[:], LIFT, mid[:], ALU.mult, ALU.add)
+        nc.vector.scalar_tensor_tensor(unshift[:], small[:], 1.0 / LIFT, mid[:], ALU.mult, ALU.add)
+        nc.vector.scalar_tensor_tensor(shift[:], large[:], DROP, shift[:], ALU.mult, ALU.add)
+        nc.vector.scalar_tensor_tensor(unshift[:], large[:], 1.0 / DROP, unshift[:], ALU.mult, ALU.add)
+        nc.vector.tensor_tensor(inner[:], size[:], shift[:], ALU.mult)
+        nc.vector.tensor_tensor(sign[:], sign[:], unshift[:], ALU.mult)
+        nc.vector.tensor_scalar(inner[:], inner[:], FLOOR, None, ALU.max)
+        nc.scalar.activation(log0[:], inner[:], ACT.Ln)
+        nc.scalar.activation(back[:], log0[:], ACT.Exp, scale=-1.0)
+        factor = []
+        for b in range(2):
+            factor.append(keep.tile([P, PIECE, PACK], BF16, name="factor%d" % b, align_bytes=64))
+            nc.vector.tensor_copy(
+                factor[b][:], sign[:, b * PACK : (b + 1) * PACK].unsqueeze(1).to_broadcast([P, PIECE, PACK])
+            )
+
+        ident = keep.tile([P, P], F32, name="ident")
+        make_identity(nc, ident[:])
+        nc.vector.tensor_tensor(back[:], back[:], inner[:], ALU.mult)
+        nc.vector.scalar_tensor_tensor(log_gain[:], back[:], -1.0, log0[:], ALU.add, ALU.add)
+
+        v = {}
+
+        def gather(a, j):
+            v[a, j] = keep.tile([P, HALF], U32, name="v%d%d" % (a, j), align_bytes=64)
+            cols = HALF // LIST
+            nc.vector.tensor_copy(v[a, j][:], tab[a][:].bitcast(U32).indirect(pick[:, j * cols : (j + 1) * cols]))
+
+        gather(0, 0)
+        gather(0, 1)
+
+        w4 = keep.tile([P, 4 * H], U8, name="w4", align_bytes=64)
+        nc.vector.tensor_copy(
+            w4[:].bitcast(U16).rearrange("p (g t m e) -> p g m t e", g=4, t=PACK, e=8),
+            w4_raw[:].bitcast(U16).rearrange("p (g m e t) -> p g m t e", g=4, t=PACK, e=8),
+        )
+        gather(1, 0)
+        gather(1, 1)
+
+        exp_a, exp_b, wb_codes, wb_plane, h_codes, h_plane = {}, {}, {}, {}, {}, {}
+
+        def cation(b, j):
+            exp_a[b, j] = keep.tile([P, PACK, HALF], F32, name="exp_a%d%d" % (b, j))
+            for t in range(PACK):
+                acc = ab_psum.tile([P, HALF], F32, name="acc", tag="acc")
+                for a in range(2):
+                    c0 = a * H + b * PASS + t * P
+                    nc.tensor.matmul_mx(
+                        out=acc[:],
+                        lhsT=w4[:, 2 * c0 : 2 * (c0 + P)].bitcast(E2M1),
+                        lhsT_scale=plane(a, W4_AT + b * PASS + t * P, P),
+                        rhs=v[a, j][:].bitcast(E4M3),
+                        rhs_scale=plane(a, V_AT + j * HALF, HALF),
+                        start=(a == 0),
+                        stop=(a == 1),
+                    )
+                col = b * PACK + t
+                nc.scalar.activation(exp_a[b, j][:, t, :], acc[:], ACT.Exp, bias=log_gain[:, col : col + 1])
+
+        def anion(b, j):
+            exp_b[b, j] = ring.tile([P, PACK, HALF], F32, name="exp_b%d%d" % (b, j), tag="exp_b")
+            for t in range(PACK):
+                acc = ab_psum.tile([P, HALF], F32, name="acc", tag="acc")
+                for a in range(2):
+                    nc.tensor.matmul_mx(
+                        out=acc[:],
+                        lhsT=wb_codes[a, b][:, t * P : (t + 1) * P].bitcast(E4M3),
+                        lhsT_scale=wb_plane[a, b][:, t * P : (t + 1) * P],
+                        rhs=v[a, j][:].bitcast(E4M3),
+                        rhs_scale=plane(a, V_AT + j * HALF, HALF),
+                        start=(a == 0),
+                        stop=(a == 1),
+                    )
+                col = b * PACK + t
+                nc.scalar.activation(exp_b[b, j][:, t, :], acc[:], ACT.Exp, bias=log_gain[:, col : col + 1])
+
+        def quantise_wb(a, b, on_vector):
+            rounded = ring.tile([P, PASS * PACK], BF16, name="rounded", tag="rounded", align_bytes=64)
+            dst = rounded[:].rearrange("p (t m i) -> p m i t", t=PACK, i=PACK)
+            src = wb_raw[a, b][:].rearrange("p i (m t) -> p m i t", t=PACK)
+            nc.vector.tensor_copy(dst[:, :on_vector], src[:, :on_vector])
+            if on_vector < P:
+                nc.scalar.copy(dst[:, on_vector:], src[:, on_vector:])
+            wb_codes[a, b] = keep.tile([P, PASS], U32, name="wb_codes%d%d" % (a, b), align_bytes=64)
+            wb_plane[a, b] = keep.tile([P, PASS], U8, name="wb_plane%d%d" % (a, b), align_bytes=64)
+            nc.vector.quantize_mx(out=wb_codes[a, b][:].bitcast(E4M3), scales=wb_plane[a, b][:], in_=rounded[:])
+
+        def features(b, j):
+            h_codes[b, j] = keep.tile([P, HALF], U32, name="h_codes%d%d" % (b, j), align_bytes=64)
+            h_plane[b, j] = keep.tile([P, HALF], U8, name="h_plane%d%d" % (b, j), align_bytes=64)
+            pieces = range(HALF // PIECE)
+            diff, h = [], []
+            for u in pieces:
+                diff.append(ring.tile([P, PIECE * PACK], BF16, name="diff", tag="diff", align_bytes=64))
+                cols = slice(u * PIECE, (u + 1) * PIECE)
+                nc.vector.tensor_tensor(
+                    diff[u][:].rearrange("p (c e t) -> p c t e", e=4, t=PACK),
+                    exp_a[b, j][:, :, cols].rearrange("p t (c e) -> p c t e", e=4),
+                    exp_b[b, j][:, :, cols].rearrange("p t (c e) -> p c t e", e=4),
+                    ALU.subtract,
+                )
+            for u in pieces:
+                h.append(ring.tile([P, PIECE * PACK], BF16, name="h", tag="h", align_bytes=64))
+                nc.vector.tensor_tensor(h[u][:], diff[u][:], factor[b][:].rearrange("p c t -> p (c t)"), ALU.mult)
+            for u in pieces:
+                cols = slice(u * PIECE, (u + 1) * PIECE)
+                nc.vector.quantize_mx(out=h_codes[b, j][:, cols].bitcast(E4M3), scales=h_plane[b, j][:, cols], in_=h[u][:])
+
+        y = {}
+        last = N // P - 1
+
+        def balance(j):
+            for n in range(N // P):
+                acc = y_psum.tile([P, HALF], F32, name="y_acc", tag="y_acc")
+                for b in range(2):
+                    nc.tensor.matmul_mx(
+                        out=acc[:],
+                        lhsT=w8[:, b, n * P : (n + 1) * P].bitcast(E4M3),
+                        lhsT_scale=plane(b, W8_AT + n * P, P),
+                        rhs=h_codes[b, j][:].bitcast(E4M3),
+                        rhs_scale=h_plane[b, j][:],
+                        start=(b == 0),
+                        stop=(b == 1),
+                    )
+                if (n, j) == (last - 1, 1):
+                    y[n, j] = keep.tile([P, HALF], F32, name="y_held", tag="held")
+                else:
+                    y[n, j] = ybuf.tile([P, HALF], F32, name="y", tag="y")
+                nc.scalar.activation(y[n, j][:], acc[:], ACT.Copy, scale=-1.0)
+
+        page = [keep.tile([P, S], F32, name="page%d" % n) for n in range(last)]
+
+        def put(n, j):
+            cols = HALF // LIST
+            nc.vector.tensor_tensor(
+                page[n][:].indirect(place[:, j * cols : (j + 1) * cols]),
+                y[n, j][:],
+                wgo_sb[:, j * HALF : (j + 1) * HALF],
+                ALU.mult,
+            )
+
+        def finish_on_tensor(n):
+            for u in range(S // HALF):
+                turned = ab_psum.tile([P, HALF], F32, name="turned", tag="acc")
+                for c in range(HALF // P):
+                    cols = slice(u * HALF + c * P, u * HALF + (c + 1) * P)
+                    block = turned[:, c * P : (c + 1) * P]
+                    nc.tensor.matmul(block, gap[:, n, cols], ident[:], start=True, stop=False, is_transpose=True)
+                    nc.tensor.matmul(block, page[n][:, cols], ident[:], start=False, stop=True, is_transpose=True)
+                if (n, u) == (last - 1, 1):
+                    size_t = keep.tile([P, HALF], F32, name="size_held", tag="tail")
+                else:
+                    size_t = ring.tile([P, HALF], F32, name="size_t", tag="size_t")
+                nc.scalar.activation(size_t[:], turned[:], ACT.Abs)
+                upright = ab_psum.tile([P, HALF], F32, name="upright", tag="acc")
+                for c in range(HALF // P):
+                    nc.tensor.transpose(upright[:, c * P : (c + 1) * P], size_t[:, c * P : (c + 1) * P], ident[:])
+                cols = slice(u * HALF, (u + 1) * HALF)
+                nc.scalar.copy(gap[:, n, cols], upright[:])
+                nc.sync.dma_start(out[n * P : (n + 1) * P, cols], gap[:, n, cols])
+
+        def finish_on_vector(n):
+            result = keep.tile([P, S], F32, name="result", tag="tail")
+            for u in range(S // PIECE):
+                cols = slice(u * PIECE, (u + 1) * PIECE)
+                nc.vector.tensor_tensor(gap[:, n, cols], gap[:, n, cols], page[n][:, cols], ALU.add)
+                nc.scalar.activation(result[:, cols], gap[:, n, cols], ACT.Abs)
+                nc.sync.dma_start(out[n * P : (n + 1) * P, cols], result[:, cols])
+
+        cation(0, 0)
+        cation(1, 0)
+        quantise_wb(0, 0, P)
+        quantise_wb(1, 0, P)
+        anion(0, 0)
+        quantise_wb(0, 1, P)
+        quantise_wb(1, 1, P)
+        anion(1, 0)
+        features(0, 0)
+        cation(0, 1)
+        anion(0, 1)
+        features(1, 0)
+        balance(0)
+        features(0, 1)
+        cation(1, 1)
+        anion(1, 1)
+        put(0, 0)
+        features(1, 1)
+        balance(1)
+        for n in range(1, last):
+            put(n, 0)
+        for n in range(last):
+            put(n, 1)
+            finish_on_tensor(n)
+        page.append(keep.tile([P, S], F32, name="page_last", tag="held"))
+        put(last, 0)
+        put(last, 1)
+        finish_on_vector(last)

@@ -29,7 +29,7 @@ V_AT, W4_AT, W8_AT, ROW = 0, S, S + H, S + H + N
 
 TINY, LIFT = 2.0**-50, 2.0**90
 HUGE, DROP = 2.0**50, 2.0**-70
-FLOOR = 2.0**-60
+FLOOR = 2.0**-126
 
 
 def tile_list_elution_balance_gap_kernel(
@@ -50,51 +50,74 @@ def tile_list_elution_balance_gap_kernel(
 
         tab_rows = keep.tile([P, T], U8, name="tab_rows", align_bytes=64)
         w4_rows = keep.tile([P, H], U8, name="w4_rows", align_bytes=64)
-        rows = keep.tile([P, ROW], U8, name="rows", align_bytes=64)
         planes = keep.tile([P, 2 * ROW], U8, name="planes", align_bytes=64)
-        for loaded in (tab_rows, w4_rows):
-            nc.vector.memset(loaded[:].bitcast(I32)[32:64, :], 0)
-            nc.vector.memset(loaded[:].bitcast(I32)[64:128, :], 0)
-        nc.gpsimd.memset(planes[:].bitcast(I32), 0)
+        rows = planes[:, :ROW]
+        for loaded in (tab_rows[:], w4_rows[:], rows[:, W8_AT:]):
+            nc.vector.memset(loaded.bitcast(I32)[32:64, :], 0)
+            nc.vector.memset(loaded.bitcast(I32)[64:128, :], 0)
+        nc.gpsimd.memset(planes[:, ROW:].bitcast(I32), 0)
 
         def plane(a, first, width):
             return planes[:, a * ROW + first : a * ROW + first + width]
 
+        gain_sb = keep.tile([P, 2 * PACK], F32, name="gain_sb")
+        nc.sync.dma_start(
+            gain_sb[:].rearrange("p (b t) -> p b t", t=PACK), gain.rearrange("(b p t) -> p b t", p=P, t=PACK)
+        )
         nc.sync.dma_start(tab_rows[:].bitcast(I32)[0:32, :], tab_scales.rearrange("a q t -> (a q) t").bitcast(I32))
         nc.sync.dma_start(pick[:], offs)
         nc.sync.dma_start(w4_rows[:].bitcast(I32)[0:32, :], w4_scales.rearrange("a q c -> (a q) c").bitcast(I32))
         nc.sync.dma_start(
             rows[:, W8_AT:].bitcast(I32)[0:32, :], w8_scales.rearrange("b q n -> (b q) n").bitcast(I32)
         )
-        gain_sb = keep.tile([P, 2 * PACK], F32, name="gain_sb")
-        nc.sync.dma_start(
-            gain_sb[:].rearrange("p (b t) -> p b t", t=PACK), gain.rearrange("(b p t) -> p b t", p=P, t=PACK)
-        )
         tab = []
         for a in range(2):
             tab.append(big.tile([P, T], I32, name="tab%d" % a, tag="wide", align_bytes=64))
         nc.sync.dma_start(tab[0][:], tab_words[0].rearrange("p t i -> p (t i)").bitcast(I32))
-        w4_raw = keep.tile([P, 4 * H], U8, name="w4_raw", align_bytes=64)
+        w4_raw = keep.tile([P, 4 * H], U8, name="w4_raw", tag="narrow", align_bytes=64)
         nc.sync.dma_start(
             w4_raw[:].bitcast(I32).rearrange("p (a c) -> p a c", a=2), w4_words.bitcast(I32).rearrange("a p c -> p a c")
         )
         nc.sync.dma_start(tab[1][:], tab_words[1].rearrange("p t i -> p (t i)").bitcast(I32))
+        nc.sync.dma_start(place[:], offs2)
         wb_raw = {}
         for b in range(2):
             for a in range(2):
-                wb_raw[a, b] = keep.tile([P, PACK, PASS], F32, name="wb_raw%d%d" % (a, b))
+                pool, tag = (keep, "narrow") if (a, b) == (1, 0) else (big, "wide")
+                wb_raw[a, b] = pool.tile([P, PACK, PASS], F32, name="wb_raw%d%d" % (a, b), tag=tag, align_bytes=64)
                 nc.sync.dma_start(
                     wb_raw[a, b][:],
                     wb[a * PASS : (a + 1) * PASS, b * PASS : (b + 1) * PASS].rearrange("(p i) c -> p i c", i=PACK),
                 )
-        w8 = keep.tile([P, 2, N], I32, name="w8", align_bytes=64)
+        w8 = keep.tile([P, 2, N], I32, name="w8", tag="narrow", align_bytes=64)
         nc.sync.dma_start(w8[:], w8_words.rearrange("b p n i -> p b (n i)").bitcast(I32))
-        nc.sync.dma_start(place[:], offs2)
-        wgo_sb = keep.tile([P, S], F32, name="wgo_sb")
+        wgo_sb = big.tile([P, S], F32, name="wgo_sb", tag="wide", align_bytes=64)
         nc.sync.dma_start(wgo_sb[:], wgo)
         gap = big.tile([P, N // P, S], F32, name="gap", tag="wide", align_bytes=64)
         for n in range(N // P):
             nc.sync.dma_start(gap[:, n, :], x0[n * P : (n + 1) * P, :])
+
+        def column(name):
+            return keep.tile([P, 2 * PACK], F32, name=name)
+
+        size, lift, drop, shift = column("size"), column("lift"), column("drop"), column("shift")
+        inner, log_gain, back, outer = column("inner"), column("log_gain"), column("back"), column("outer")
+        nc.vector.scalar_tensor_tensor(size[:], gain_sb[:], -1.0, gain_sb[:], ALU.mult, ALU.max)
+        nc.vector.tensor_scalar(lift[:], size[:], TINY, LIFT, ALU.is_lt, ALU.mult)
+        nc.vector.tensor_scalar(drop[:], size[:], HUGE, LIFT, ALU.is_le, ALU.mult)
+        nc.vector.tensor_scalar(lift[:], lift[:], 1.0, None, ALU.max)
+        nc.vector.scalar_tensor_tensor(shift[:], drop[:], DROP, lift[:], ALU.max, ALU.min)
+        nc.vector.scalar_tensor_tensor(inner[:], size[:], FLOOR, shift[:], ALU.max, ALU.mult)
+        nc.scalar.activation(log_gain[:], inner[:], ACT.Ln)
+        nc.scalar.activation(back[:], log_gain[:], ACT.Exp, scale=-1.0)
+        nc.gpsimd.tensor_tensor(outer[:], gain_sb[:], back[:], ALU.mult)
+
+        factor = []
+        for b in range(2):
+            factor.append(keep.tile([P, PIECE, PACK], BF16, name="factor%d" % b, align_bytes=64))
+            nc.scalar.activation(
+                factor[b][:], outer[:, b * PACK : (b + 1) * PACK].unsqueeze(1).to_broadcast([P, PIECE, PACK]), ACT.Copy
+            )
 
         v_rows = keep.tile([P, S], U8, name="v_rows", align_bytes=64)
         nc.vector.tensor_copy(v_rows[:], tab_rows[:].indirect(pick[:]))
@@ -104,44 +127,13 @@ def tile_list_elution_balance_gap_kernel(
         )
         nc.vector.tensor_copy(rows[:, V_AT:W4_AT].bitcast(I32), v_rows[:].bitcast(I32))
         for a in range(2):
-            for q in range(QUADS):
+            for q in range(1 - a, QUADS):
                 row = 16 * a + 4 * q
-                nc.gpsimd.dma_start(
-                    plane(a, 0, ROW).bitcast(I32)[32 * q : 32 * q + 4, :], rows[:].bitcast(I32)[row : row + 4, :]
+                nc.scalar.dma_start(
+                    plane(a, 0, ROW).bitcast(I32)[32 * q : 32 * q + 4, :], rows.bitcast(I32)[row : row + 4, :]
                 )
-        def column(name):
-            return keep.tile([P, 2 * PACK], F32, name=name)
-
-        size, small, large, mid = column("size"), column("small"), column("large"), column("mid")
-        shift, unshift, sign, inner = column("shift"), column("unshift"), column("sign"), column("inner")
-        log0, back, log_gain = column("log0"), column("back"), column("log_gain")
-        nc.vector.scalar_tensor_tensor(size[:], gain_sb[:], -1.0, gain_sb[:], ALU.mult, ALU.max)
-        nc.vector.tensor_scalar(small[:], size[:], TINY, None, ALU.is_lt)
-        nc.vector.tensor_scalar(large[:], size[:], HUGE, None, ALU.is_gt)
-        nc.vector.tensor_scalar(sign[:], gain_sb[:], 0.0, None, ALU.is_lt)
-        nc.vector.scalar_tensor_tensor(mid[:], small[:], -1.0, large[:], ALU.mult, ALU.subtract)
-        nc.vector.scalar_tensor_tensor(sign[:], gain_sb[:], 0.0, sign[:], ALU.is_gt, ALU.subtract)
-        nc.vector.tensor_scalar(mid[:], mid[:], 1.0, None, ALU.add)
-        nc.vector.scalar_tensor_tensor(shift[:], small[:], LIFT, mid[:], ALU.mult, ALU.add)
-        nc.vector.scalar_tensor_tensor(unshift[:], small[:], 1.0 / LIFT, mid[:], ALU.mult, ALU.add)
-        nc.vector.scalar_tensor_tensor(shift[:], large[:], DROP, shift[:], ALU.mult, ALU.add)
-        nc.vector.scalar_tensor_tensor(unshift[:], large[:], 1.0 / DROP, unshift[:], ALU.mult, ALU.add)
-        nc.vector.tensor_tensor(inner[:], size[:], shift[:], ALU.mult)
-        nc.vector.tensor_tensor(sign[:], sign[:], unshift[:], ALU.mult)
-        nc.vector.tensor_scalar(inner[:], inner[:], FLOOR, None, ALU.max)
-        nc.scalar.activation(log0[:], inner[:], ACT.Ln)
-        nc.scalar.activation(back[:], log0[:], ACT.Exp, scale=-1.0)
-        factor = []
-        for b in range(2):
-            factor.append(keep.tile([P, PIECE, PACK], BF16, name="factor%d" % b, align_bytes=64))
-            nc.vector.tensor_copy(
-                factor[b][:], sign[:, b * PACK : (b + 1) * PACK].unsqueeze(1).to_broadcast([P, PIECE, PACK])
-            )
-
         ident = keep.tile([P, P], F32, name="ident")
         make_identity(nc, ident[:])
-        nc.vector.tensor_tensor(back[:], back[:], inner[:], ALU.mult)
-        nc.vector.scalar_tensor_tensor(log_gain[:], back[:], -1.0, log0[:], ALU.add, ALU.add)
 
         v = {}
 
@@ -200,11 +192,11 @@ def tile_list_elution_balance_gap_kernel(
 
         def quantise_wb(a, b, on_vector):
             rounded = ring.tile([P, PASS * PACK], BF16, name="rounded", tag="rounded", align_bytes=64)
-            dst = rounded[:].rearrange("p (t m i) -> p m i t", t=PACK, i=PACK)
-            src = wb_raw[a, b][:].rearrange("p i (m t) -> p m i t", t=PACK)
-            nc.vector.tensor_copy(dst[:, :on_vector], src[:, :on_vector])
+            dst = rounded[:].rearrange("p (s e m i) -> p s m i e", s=2, e=2, i=PACK)
+            src = wb_raw[a, b][:].rearrange("p i (m s e) -> p s m i e", s=2, e=2)
+            nc.vector.tensor_copy(dst[:, :, :on_vector], src[:, :, :on_vector])
             if on_vector < P:
-                nc.scalar.copy(dst[:, on_vector:], src[:, on_vector:])
+                nc.scalar.copy(dst[:, :, on_vector:], src[:, :, on_vector:])
             wb_codes[a, b] = keep.tile([P, PASS], U32, name="wb_codes%d%d" % (a, b), align_bytes=64)
             wb_plane[a, b] = keep.tile([P, PASS], U8, name="wb_plane%d%d" % (a, b), align_bytes=64)
             nc.vector.quantize_mx(out=wb_codes[a, b][:].bitcast(E4M3), scales=wb_plane[a, b][:], in_=rounded[:])
@@ -218,9 +210,9 @@ def tile_list_elution_balance_gap_kernel(
                 diff.append(ring.tile([P, PIECE * PACK], BF16, name="diff", tag="diff", align_bytes=64))
                 cols = slice(u * PIECE, (u + 1) * PIECE)
                 nc.vector.tensor_tensor(
-                    diff[u][:].rearrange("p (c e t) -> p c t e", e=4, t=PACK),
-                    exp_a[b, j][:, :, cols].rearrange("p t (c e) -> p c t e", e=4),
-                    exp_b[b, j][:, :, cols].rearrange("p t (c e) -> p c t e", e=4),
+                    diff[u][:].rearrange("p (c e t) -> p c t e", e=2, t=PACK),
+                    exp_a[b, j][:, :, cols].rearrange("p t (c e) -> p c t e", e=2),
+                    exp_b[b, j][:, :, cols].rearrange("p t (c e) -> p c t e", e=2),
                     ALU.subtract,
                 )
             for u in pieces:
@@ -265,7 +257,7 @@ def tile_list_elution_balance_gap_kernel(
 
         def finish_on_tensor(n):
             for u in range(S // HALF):
-                turned = ab_psum.tile([P, HALF], F32, name="turned", tag="acc")
+                turned = y_psum.tile([P, HALF], F32, name="turned", tag="y_acc")
                 for c in range(HALF // P):
                     cols = slice(u * HALF + c * P, u * HALF + (c + 1) * P)
                     block = turned[:, c * P : (c + 1) * P]
@@ -276,7 +268,7 @@ def tile_list_elution_balance_gap_kernel(
                 else:
                     size_t = ring.tile([P, HALF], F32, name="size_t", tag="size_t")
                 nc.scalar.activation(size_t[:], turned[:], ACT.Abs)
-                upright = ab_psum.tile([P, HALF], F32, name="upright", tag="acc")
+                upright = y_psum.tile([P, HALF], F32, name="upright", tag="y_acc")
                 for c in range(HALF // P):
                     nc.tensor.transpose(upright[:, c * P : (c + 1) * P], size_t[:, c * P : (c + 1) * P], ident[:])
                 cols = slice(u * HALF, (u + 1) * HALF)
@@ -297,7 +289,7 @@ def tile_list_elution_balance_gap_kernel(
         quantise_wb(1, 0, P)
         anion(0, 0)
         quantise_wb(0, 1, P)
-        quantise_wb(1, 1, P)
+        quantise_wb(1, 1, P // 2)
         anion(1, 0)
         features(0, 0)
         cation(0, 1)

@@ -41,7 +41,6 @@ def tile_list_elution_balance_gap_kernel(
         keep = ctx.enter_context(tc.tile_pool(name="keep", bufs=1))
         big = ctx.enter_context(tc.tile_pool(name="big", bufs=2))
         ring = ctx.enter_context(tc.tile_pool(name="ring", bufs=2))
-        ybuf = ctx.enter_context(tc.tile_pool(name="ybuf", bufs=7))
         ab_psum = ctx.enter_context(tc.psum_pool(name="ab_psum", bufs=6))
         y_psum = ctx.enter_context(tc.psum_pool(name="y_psum", bufs=2))
 
@@ -80,13 +79,14 @@ def tile_list_elution_balance_gap_kernel(
         )
         nc.sync.dma_start(tab[1][:], tab_words[1].rearrange("p t i -> p (t i)").bitcast(I32))
         nc.sync.dma_start(place[:], offs2)
-        wb_raw = {}
+        wb_first = big.tile([P, 2, PACK, PASS], F32, name="wb_first", tag="wide", align_bytes=64)
+        wb_third = keep.tile([P, PACK, PASS], F32, name="wb_third", tag="narrow", align_bytes=64)
+        wb_fourth = big.tile([P, PACK, PASS], F32, name="wb_fourth", tag="wide", align_bytes=64)
+        wb_raw = {(0, 0): wb_first[:, 0], (1, 0): wb_first[:, 1], (0, 1): wb_third[:], (1, 1): wb_fourth[:]}
         for b in range(2):
             for a in range(2):
-                pool, tag = (keep, "narrow") if (a, b) == (1, 0) else (big, "wide")
-                wb_raw[a, b] = pool.tile([P, PACK, PASS], F32, name="wb_raw%d%d" % (a, b), tag=tag, align_bytes=64)
                 nc.sync.dma_start(
-                    wb_raw[a, b][:],
+                    wb_raw[a, b],
                     wb[a * PASS : (a + 1) * PASS, b * PASS : (b + 1) * PASS].rearrange("(p i) c -> p i c", i=PACK),
                 )
         w8 = keep.tile([P, 2, N], I32, name="w8", tag="narrow", align_bytes=64)
@@ -156,7 +156,7 @@ def tile_list_elution_balance_gap_kernel(
         exp_a, exp_b, wb_codes, wb_plane, h_codes, h_plane = {}, {}, {}, {}, {}, {}
 
         def cation(b, j):
-            exp_a[b, j] = keep.tile([P, PACK, HALF], F32, name="exp_a%d%d" % (b, j))
+            exp_a[b, j] = keep.tile([P, PACK, HALF], F32, name="exp_a%d%d" % (b, j), tag="exp_a%d%d" % (b, j))
             for t in range(PACK):
                 acc = ab_psum.tile([P, HALF], F32, name="acc", tag="acc")
                 for a in range(2):
@@ -193,7 +193,7 @@ def tile_list_elution_balance_gap_kernel(
         def quantise_wb(a, b, on_vector):
             rounded = ring.tile([P, PASS * PACK], BF16, name="rounded", tag="rounded", align_bytes=64)
             dst = rounded[:].rearrange("p (s e m i) -> p s m i e", s=2, e=2, i=PACK)
-            src = wb_raw[a, b][:].rearrange("p i (m s e) -> p s m i e", s=2, e=2)
+            src = wb_raw[a, b].rearrange("p i (m s e) -> p s m i e", s=2, e=2)
             nc.vector.tensor_copy(dst[:, :, :on_vector], src[:, :, :on_vector])
             if on_vector < P:
                 nc.scalar.copy(dst[:, :, on_vector:], src[:, :, on_vector:])
@@ -207,7 +207,7 @@ def tile_list_elution_balance_gap_kernel(
             pieces = range(HALF // PIECE)
             diff, h = [], []
             for u in pieces:
-                diff.append(ring.tile([P, PIECE * PACK], BF16, name="diff", tag="diff", align_bytes=64))
+                diff.append(ring.tile([P, PIECE * PACK], BF16, name="diff", tag="rounded", align_bytes=64))
                 cols = slice(u * PIECE, (u + 1) * PIECE)
                 nc.vector.tensor_tensor(
                     diff[u][:].rearrange("p (c e t) -> p c t e", e=2, t=PACK),
@@ -223,35 +223,35 @@ def tile_list_elution_balance_gap_kernel(
                 nc.vector.quantize_mx(out=h_codes[b, j][:, cols].bitcast(E4M3), scales=h_plane[b, j][:, cols], in_=h[u][:])
 
         y = {}
+        for n, j in ((0, 0), (0, 1), (1, 0), (1, 1)):
+            y[n, j] = keep.tile([P, HALF], F32, name="y%d%d" % (n, j), tag="y%d%d" % (n, j))[:]
+        for n in (2, 3):
+            y[n] = keep.tile([P, S], F32, name="y%d" % n, tag="y%d" % n)[:]
+            for j in range(2):
+                y[n, j] = y[n][:, j * HALF : (j + 1) * HALF]
         last = N // P - 1
 
-        def balance(j):
-            for n in range(N // P):
-                acc = y_psum.tile([P, HALF], F32, name="y_acc", tag="y_acc")
-                for b in range(2):
-                    nc.tensor.matmul_mx(
-                        out=acc[:],
-                        lhsT=w8[:, b, n * P : (n + 1) * P].bitcast(E4M3),
-                        lhsT_scale=plane(b, W8_AT + n * P, P),
-                        rhs=h_codes[b, j][:].bitcast(E4M3),
-                        rhs_scale=h_plane[b, j][:],
-                        start=(b == 0),
-                        stop=(b == 1),
-                    )
-                if (n, j) == (last - 1, 1):
-                    y[n, j] = keep.tile([P, HALF], F32, name="y_held", tag="held")
-                else:
-                    y[n, j] = ybuf.tile([P, HALF], F32, name="y", tag="y")
-                nc.scalar.activation(y[n, j][:], acc[:], ACT.Copy, scale=-1.0)
+        def balance(n, j):
+            acc = y_psum.tile([P, HALF], F32, name="y_acc", tag="y_acc")
+            for b in range(2):
+                nc.tensor.matmul_mx(
+                    out=acc[:],
+                    lhsT=w8[:, b, n * P : (n + 1) * P].bitcast(E4M3),
+                    lhsT_scale=plane(b, W8_AT + n * P, P),
+                    rhs=h_codes[b, j][:].bitcast(E4M3),
+                    rhs_scale=h_plane[b, j][:],
+                    start=(b == 0),
+                    stop=(b == 1),
+                )
+            nc.scalar.activation(y[n, j], acc[:], ACT.Copy, scale=-1.0)
 
-        page = [keep.tile([P, S], F32, name="page%d" % n) for n in range(last)]
+        page = {}
 
-        def put(n, j):
-            cols = HALF // LIST
+        def put(n, first, count):
             nc.vector.tensor_tensor(
-                page[n][:].indirect(place[:, j * cols : (j + 1) * cols]),
-                y[n, j][:],
-                wgo_sb[:, j * HALF : (j + 1) * HALF],
+                page[n][:].indirect(place[:, first // LIST : (first + count) // LIST]),
+                y[n, first // HALF] if count == HALF else y[n],
+                wgo_sb[:, first : first + count],
                 ALU.mult,
             )
 
@@ -295,19 +295,27 @@ def tile_list_elution_balance_gap_kernel(
         cation(0, 1)
         anion(0, 1)
         features(1, 0)
-        balance(0)
+        balance(0, 0)
         features(0, 1)
         cation(1, 1)
         anion(1, 1)
-        put(0, 0)
+        page[0] = keep.tile([P, S], F32, name="page0")
+        put(0, 0, HALF)
+        balance(1, 0)
         features(1, 1)
-        balance(1)
-        for n in range(1, last):
-            put(n, 0)
-        for n in range(last):
-            put(n, 1)
+        balance(0, 1)
+        balance(1, 1)
+        for n in range(2, N // P):
+            balance(n, 0)
+            balance(n, 1)
+        page[1] = keep.tile([P, S], F32, name="page1", tag="exp_a11")
+        put(1, 0, HALF)
+        for n in range(2):
+            put(n, HALF, HALF)
             finish_on_tensor(n)
-        page.append(keep.tile([P, S], F32, name="page_last", tag="held"))
-        put(last, 0)
-        put(last, 1)
+        page[2] = keep.tile([P, 2 * S], F32, name="page2", tag="y11")
+        put(2, 0, S)
+        finish_on_tensor(2)
+        page[3] = keep.tile([P, 2 * S], F32, name="page3", tag="y2")
+        put(3, 0, S)
         finish_on_vector(last)

@@ -20,10 +20,14 @@ ACT = mybir.ActivationFunctionType
 P = 128
 PACK = 4
 PASS = P * PACK
+PASSES = 2
 QUADS = 4
+QUAD = P // QUADS
+BLOCKS = PASS // 32
 HALF = 512
 PIECE = 256
 LIST = 16
+PAGES = N // P
 
 V_AT, W4_AT, W8_AT, ROW = 0, S, S + H, S + H + N
 
@@ -47,58 +51,65 @@ def tile_list_elution_balance_gap_kernel(
         pick = lists.tile([P, S // LIST], U16, name="pick")
         place = lists.tile([P, S // LIST], U16, name="place")
 
+        scale_rows = PASSES * BLOCKS
         tab_rows = keep.tile([P, T], U8, name="tab_rows", align_bytes=64)
         w4_rows = keep.tile([P, H], U8, name="w4_rows", align_bytes=64)
-        planes = keep.tile([P, 2 * ROW], U8, name="planes", align_bytes=64)
+        planes = keep.tile([P, PASSES * ROW], U8, name="planes", align_bytes=64)
         rows = planes[:, :ROW]
         for loaded in (tab_rows[:], w4_rows[:], rows[:, W8_AT:]):
-            nc.vector.memset(loaded.bitcast(I32)[32:64, :], 0)
-            nc.vector.memset(loaded.bitcast(I32)[64:128, :], 0)
+            nc.vector.memset(loaded.bitcast(I32)[scale_rows : P // 2, :], 0)
+            nc.vector.memset(loaded.bitcast(I32)[P // 2 : P, :], 0)
         nc.gpsimd.memset(planes[:, ROW:].bitcast(I32), 0)
 
-        def plane(a, first, width):
-            return planes[:, a * ROW + first : a * ROW + first + width]
+        def plane(g, first, width):
+            return planes[:, g * ROW + first : g * ROW + first + width]
 
-        gain_sb = keep.tile([P, 2 * PACK], F32, name="gain_sb")
+        gain_sb = keep.tile([P, PASSES * PACK], F32, name="gain_sb")
         nc.sync.dma_start(
             gain_sb[:].rearrange("p (b t) -> p b t", t=PACK), gain.rearrange("(b p t) -> p b t", p=P, t=PACK)
         )
-        nc.sync.dma_start(tab_rows[:].bitcast(I32)[0:32, :], tab_scales.rearrange("a q t -> (a q) t").bitcast(I32))
-        nc.sync.dma_start(pick[:], offs)
-        nc.sync.dma_start(w4_rows[:].bitcast(I32)[0:32, :], w4_scales.rearrange("a q c -> (a q) c").bitcast(I32))
         nc.sync.dma_start(
-            rows[:, W8_AT:].bitcast(I32)[0:32, :], w8_scales.rearrange("b q n -> (b q) n").bitcast(I32)
+            tab_rows[:].bitcast(I32)[0:scale_rows, :], tab_scales.rearrange("a q t -> (a q) t").bitcast(I32)
+        )
+        nc.sync.dma_start(pick[:], offs)
+        nc.sync.dma_start(
+            w4_rows[:].bitcast(I32)[0:scale_rows, :], w4_scales.rearrange("a q c -> (a q) c").bitcast(I32)
+        )
+        nc.sync.dma_start(
+            rows[:, W8_AT:].bitcast(I32)[0:scale_rows, :], w8_scales.rearrange("b q n -> (b q) n").bitcast(I32)
         )
         tab = []
-        for a in range(2):
+        for a in range(PASSES):
             tab.append(big.tile([P, T], I32, name="tab%d" % a, tag="wide", align_bytes=64))
         nc.sync.dma_start(tab[0][:], tab_words[0].rearrange("p t i -> p (t i)").bitcast(I32))
         w4_raw = keep.tile([P, 4 * H], U8, name="w4_raw", tag="narrow", align_bytes=64)
         nc.sync.dma_start(
-            w4_raw[:].bitcast(I32).rearrange("p (a c) -> p a c", a=2), w4_words.bitcast(I32).rearrange("a p c -> p a c")
+            w4_raw[:].bitcast(I32).rearrange("p (a c) -> p a c", a=PASSES),
+            w4_words.bitcast(I32).rearrange("a p c -> p a c"),
         )
-        nc.sync.dma_start(tab[1][:], tab_words[1].rearrange("p t i -> p (t i)").bitcast(I32))
         nc.sync.dma_start(place[:], offs2)
-        wb_first = big.tile([P, 2, PACK, PASS], F32, name="wb_first", tag="wide", align_bytes=64)
+        nc.sync.dma_start(tab[1][:], tab_words[1].rearrange("p t i -> p (t i)").bitcast(I32))
+
+        wb_first = big.tile([P, PASSES, PACK, PASS], F32, name="wb_first", tag="wide", align_bytes=64)
         wb_third = keep.tile([P, PACK, PASS], F32, name="wb_third", tag="narrow", align_bytes=64)
         wb_fourth = big.tile([P, PACK, PASS], F32, name="wb_fourth", tag="wide", align_bytes=64)
         wb_raw = {(0, 0): wb_first[:, 0], (1, 0): wb_first[:, 1], (0, 1): wb_third[:], (1, 1): wb_fourth[:]}
-        for b in range(2):
-            for a in range(2):
+        for b in range(PASSES):
+            for a in range(PASSES):
                 nc.sync.dma_start(
                     wb_raw[a, b],
                     wb[a * PASS : (a + 1) * PASS, b * PASS : (b + 1) * PASS].rearrange("(p i) c -> p i c", i=PACK),
                 )
-        w8 = keep.tile([P, 2, N], I32, name="w8", tag="narrow", align_bytes=64)
+        w8 = keep.tile([P, PASSES, N], I32, name="w8", tag="narrow", align_bytes=64)
         nc.sync.dma_start(w8[:], w8_words.rearrange("b p n i -> p b (n i)").bitcast(I32))
         wgo_sb = big.tile([P, S], F32, name="wgo_sb", tag="wide", align_bytes=64)
         nc.sync.dma_start(wgo_sb[:], wgo)
-        gap = big.tile([P, N // P, S], F32, name="gap", tag="wide", align_bytes=64)
-        for n in range(N // P):
+        gap = big.tile([P, PAGES, S], F32, name="gap", tag="wide", align_bytes=64)
+        for n in range(PAGES):
             nc.sync.dma_start(gap[:, n, :], x0[n * P : (n + 1) * P, :])
 
         def column(name):
-            return keep.tile([P, 2 * PACK], F32, name=name)
+            return keep.tile([P, PASSES * PACK], F32, name=name)
 
         size, lift, drop, shift = column("size"), column("lift"), column("drop"), column("shift")
         inner, log_gain, back, outer = column("inner"), column("log_gain"), column("back"), column("outer")
@@ -110,10 +121,10 @@ def tile_list_elution_balance_gap_kernel(
         nc.vector.scalar_tensor_tensor(inner[:], size[:], FLOOR, shift[:], ALU.max, ALU.mult)
         nc.scalar.activation(log_gain[:], inner[:], ACT.Ln)
         nc.scalar.activation(back[:], log_gain[:], ACT.Exp, scale=-1.0)
-        nc.gpsimd.tensor_tensor(outer[:], gain_sb[:], back[:], ALU.mult)
+        nc.vector.tensor_tensor(outer[:], gain_sb[:], back[:], ALU.mult)
 
         factor = []
-        for b in range(2):
+        for b in range(PASSES):
             factor.append(keep.tile([P, PIECE, PACK], BF16, name="factor%d" % b, align_bytes=64))
             nc.scalar.activation(
                 factor[b][:], outer[:, b * PACK : (b + 1) * PACK].unsqueeze(1).to_broadcast([P, PIECE, PACK]), ACT.Copy
@@ -122,16 +133,17 @@ def tile_list_elution_balance_gap_kernel(
         v_rows = keep.tile([P, S], U8, name="v_rows", align_bytes=64)
         nc.vector.tensor_copy(v_rows[:], tab_rows[:].indirect(pick[:]))
         nc.vector.tensor_copy(
-            rows[:, W4_AT:W8_AT].rearrange("p (b t m e) -> p b m t e", b=2, t=PACK, e=16),
-            w4_rows[:].rearrange("p (b m e t) -> p b m t e", b=2, t=PACK, e=16),
+            rows[:, W4_AT:W8_AT].rearrange("p (b t m e) -> p b m t e", b=PASSES, t=PACK, e=16),
+            w4_rows[:].rearrange("p (b m e t) -> p b m t e", b=PASSES, t=PACK, e=16),
         )
         nc.vector.tensor_copy(rows[:, V_AT:W4_AT].bitcast(I32), v_rows[:].bitcast(I32))
-        for a in range(2):
-            for q in range(1 - a, QUADS):
-                row = 16 * a + 4 * q
-                nc.scalar.dma_start(
-                    plane(a, 0, ROW).bitcast(I32)[32 * q : 32 * q + 4, :], rows.bitcast(I32)[row : row + 4, :]
-                )
+        moves = [(g, q) for g in range(PASSES) for q in range(QUADS)][1:]
+        for g, q in moves:
+            row = BLOCKS * g + 4 * q
+            queue = nc.gpsimd if (g, q) == moves[0] else nc.scalar
+            queue.dma_start(
+                plane(g, 0, ROW).bitcast(I32)[QUAD * q : QUAD * q + 4, :], rows.bitcast(I32)[row : row + 4, :]
+            )
         ident = keep.tile([P, P], F32, name="ident")
         make_identity(nc, ident[:])
 
@@ -159,16 +171,16 @@ def tile_list_elution_balance_gap_kernel(
             exp_a[b, j] = keep.tile([P, PACK, HALF], F32, name="exp_a%d%d" % (b, j), tag="exp_a%d%d" % (b, j))
             for t in range(PACK):
                 acc = ab_psum.tile([P, HALF], F32, name="acc", tag="acc")
-                for a in range(2):
-                    c0 = a * H + b * PASS + t * P
+                for a in range(PASSES):
+                    first = a * H + b * PASS + t * P
                     nc.tensor.matmul_mx(
                         out=acc[:],
-                        lhsT=w4[:, 2 * c0 : 2 * (c0 + P)].bitcast(E2M1),
+                        lhsT=w4[:, 2 * first : 2 * (first + P)].bitcast(E2M1),
                         lhsT_scale=plane(a, W4_AT + b * PASS + t * P, P),
                         rhs=v[a, j][:].bitcast(E4M3),
                         rhs_scale=plane(a, V_AT + j * HALF, HALF),
                         start=(a == 0),
-                        stop=(a == 1),
+                        stop=(a == PASSES - 1),
                     )
                 col = b * PACK + t
                 nc.scalar.activation(exp_a[b, j][:, t, :], acc[:], ACT.Exp, bias=log_gain[:, col : col + 1])
@@ -177,7 +189,7 @@ def tile_list_elution_balance_gap_kernel(
             exp_b[b, j] = ring.tile([P, PACK, HALF], F32, name="exp_b%d%d" % (b, j), tag="exp_b")
             for t in range(PACK):
                 acc = ab_psum.tile([P, HALF], F32, name="acc", tag="acc")
-                for a in range(2):
+                for a in range(PASSES):
                     nc.tensor.matmul_mx(
                         out=acc[:],
                         lhsT=wb_codes[a, b][:, t * P : (t + 1) * P].bitcast(E4M3),
@@ -185,7 +197,7 @@ def tile_list_elution_balance_gap_kernel(
                         rhs=v[a, j][:].bitcast(E4M3),
                         rhs_scale=plane(a, V_AT + j * HALF, HALF),
                         start=(a == 0),
-                        stop=(a == 1),
+                        stop=(a == PASSES - 1),
                     )
                 col = b * PACK + t
                 nc.scalar.activation(exp_b[b, j][:, t, :], acc[:], ACT.Exp, bias=log_gain[:, col : col + 1])
@@ -220,20 +232,22 @@ def tile_list_elution_balance_gap_kernel(
                 nc.vector.tensor_tensor(h[u][:], diff[u][:], factor[b][:].rearrange("p c t -> p (c t)"), ALU.mult)
             for u in pieces:
                 cols = slice(u * PIECE, (u + 1) * PIECE)
-                nc.vector.quantize_mx(out=h_codes[b, j][:, cols].bitcast(E4M3), scales=h_plane[b, j][:, cols], in_=h[u][:])
+                nc.vector.quantize_mx(
+                    out=h_codes[b, j][:, cols].bitcast(E4M3), scales=h_plane[b, j][:, cols], in_=h[u][:]
+                )
 
         y = {}
         for n, j in ((0, 0), (0, 1), (1, 0), (1, 1)):
             y[n, j] = keep.tile([P, HALF], F32, name="y%d%d" % (n, j), tag="y%d%d" % (n, j))[:]
         for n in (2, 3):
             y[n] = keep.tile([P, S], F32, name="y%d" % n, tag="y%d" % n)[:]
-            for j in range(2):
+            for j in range(S // HALF):
                 y[n, j] = y[n][:, j * HALF : (j + 1) * HALF]
-        last = N // P - 1
+        last = PAGES - 1
 
         def balance(n, j):
             acc = y_psum.tile([P, HALF], F32, name="y_acc", tag="y_acc")
-            for b in range(2):
+            for b in range(PASSES):
                 nc.tensor.matmul_mx(
                     out=acc[:],
                     lhsT=w8[:, b, n * P : (n + 1) * P].bitcast(E4M3),
@@ -241,7 +255,7 @@ def tile_list_elution_balance_gap_kernel(
                     rhs=h_codes[b, j][:].bitcast(E4M3),
                     rhs_scale=h_plane[b, j][:],
                     start=(b == 0),
-                    stop=(b == 1),
+                    stop=(b == PASSES - 1),
                 )
             nc.scalar.activation(y[n, j], acc[:], ACT.Copy, scale=-1.0)
 
@@ -263,7 +277,7 @@ def tile_list_elution_balance_gap_kernel(
                     block = turned[:, c * P : (c + 1) * P]
                     nc.tensor.matmul(block, gap[:, n, cols], ident[:], start=True, stop=False, is_transpose=True)
                     nc.tensor.matmul(block, page[n][:, cols], ident[:], start=False, stop=True, is_transpose=True)
-                if (n, u) == (last - 1, 1):
+                if (n, u) == (last - 1, S // HALF - 1):
                     size_t = keep.tile([P, HALF], F32, name="size_held", tag="tail")
                 else:
                     size_t = ring.tile([P, HALF], F32, name="size_t", tag="size_t")
@@ -305,7 +319,7 @@ def tile_list_elution_balance_gap_kernel(
         features(1, 1)
         balance(0, 1)
         balance(1, 1)
-        for n in range(2, N // P):
+        for n in range(2, PAGES):
             balance(n, 0)
             balance(n, 1)
         page[1] = keep.tile([P, S], F32, name="page1", tag="exp_a11")

@@ -258,15 +258,14 @@ def tile_list_elution_balance_gap_kernel(
                     stop=(b == PASSES - 1),
                 )
             nc.scalar.activation(y[n, j], acc[:], ACT.Copy, scale=-1.0)
+            nc.gpsimd.tensor_tensor(y[n, j], y[n, j], wgo_sb[:, j * HALF : (j + 1) * HALF], ALU.mult)
 
         page = {}
 
         def put(n, first, count):
-            nc.vector.tensor_tensor(
+            nc.vector.tensor_copy(
                 page[n][:].indirect(place[:, first // LIST : (first + count) // LIST]),
                 y[n, first // HALF] if count == HALF else y[n],
-                wgo_sb[:, first : first + count],
-                ALU.mult,
             )
 
         def finish_on_tensor(n):

@@ -1,7 +1,6 @@
 from contextlib import ExitStack
 
 import concourse.mybir as mybir
-from concourse.masks import make_identity
 
 K, T, S, H, N = 1024, 4096, 1024, 1024, 512
 FLOPS = 2 * (2 * K * H * S + H * N * S)
@@ -45,8 +44,7 @@ def tile_list_elution_balance_gap_kernel(
         keep = ctx.enter_context(tc.tile_pool(name="keep", bufs=1))
         big = ctx.enter_context(tc.tile_pool(name="big", bufs=2))
         ring = ctx.enter_context(tc.tile_pool(name="ring", bufs=2))
-        ab_psum = ctx.enter_context(tc.psum_pool(name="ab_psum", bufs=6))
-        y_psum = ctx.enter_context(tc.psum_pool(name="y_psum", bufs=2))
+        psum = ctx.enter_context(tc.psum_pool(name="psum", bufs=4))
 
         pick = lists.tile([P, S // LIST], U16, name="pick")
         place = lists.tile([P, S // LIST], U16, name="place")
@@ -123,11 +121,10 @@ def tile_list_elution_balance_gap_kernel(
         nc.scalar.activation(back[:], log_gain[:], ACT.Exp, scale=-1.0)
         nc.vector.tensor_tensor(outer[:], gain_sb[:], back[:], ALU.mult)
 
-        factor = []
+        factor = keep.tile([P, PASSES, PIECE, PACK], BF16, name="factor", align_bytes=64)
         for b in range(PASSES):
-            factor.append(keep.tile([P, PIECE, PACK], BF16, name="factor%d" % b, align_bytes=64))
             nc.scalar.activation(
-                factor[b][:], outer[:, b * PACK : (b + 1) * PACK].unsqueeze(1).to_broadcast([P, PIECE, PACK]), ACT.Copy
+                factor[:, b], outer[:, b * PACK : (b + 1) * PACK].unsqueeze(1).to_broadcast([P, PIECE, PACK]), ACT.Copy
             )
 
         v_rows = keep.tile([P, S], U8, name="v_rows", align_bytes=64)
@@ -144,8 +141,6 @@ def tile_list_elution_balance_gap_kernel(
             queue.dma_start(
                 plane(g, 0, ROW).bitcast(I32)[QUAD * q : QUAD * q + 4, :], rows.bitcast(I32)[row : row + 4, :]
             )
-        ident = keep.tile([P, P], F32, name="ident")
-        make_identity(nc, ident[:])
 
         v = {}
 
@@ -165,12 +160,12 @@ def tile_list_elution_balance_gap_kernel(
         gather(1, 0)
         gather(1, 1)
 
-        exp_a, exp_b, wb_codes, wb_plane, h_codes, h_plane = {}, {}, {}, {}, {}, {}
+        exp_a, exp_b, wb_codes, wb_plane, h_codes, h_plane, h_piece = {}, {}, {}, {}, {}, {}, {}
 
-        def cation(b, j):
+        def cation(b, j, banks):
             exp_a[b, j] = keep.tile([P, PACK, HALF], F32, name="exp_a%d%d" % (b, j), tag="exp_a%d%d" % (b, j))
             for t in range(PACK):
-                acc = ab_psum.tile([P, HALF], F32, name="acc", tag="acc")
+                acc = psum.tile([P, HALF], F32, name="acc", tag=banks)
                 for a in range(PASSES):
                     first = a * H + b * PASS + t * P
                     nc.tensor.matmul_mx(
@@ -185,10 +180,10 @@ def tile_list_elution_balance_gap_kernel(
                 col = b * PACK + t
                 nc.scalar.activation(exp_a[b, j][:, t, :], acc[:], ACT.Exp, bias=log_gain[:, col : col + 1])
 
-        def anion(b, j):
-            exp_b[b, j] = ring.tile([P, PACK, HALF], F32, name="exp_b%d%d" % (b, j), tag="exp_b")
+        def anion(b, j, banks):
+            exp_b[b, j] = keep.tile([P, PACK, HALF], F32, name="exp_b%d%d" % (b, j))
             for t in range(PACK):
-                acc = ab_psum.tile([P, HALF], F32, name="acc", tag="acc")
+                acc = psum.tile([P, HALF], F32, name="acc", tag=banks)
                 for a in range(PASSES):
                     nc.tensor.matmul_mx(
                         out=acc[:],
@@ -203,7 +198,10 @@ def tile_list_elution_balance_gap_kernel(
                 nc.scalar.activation(exp_b[b, j][:, t, :], acc[:], ACT.Exp, bias=log_gain[:, col : col + 1])
 
         def quantise_wb(a, b, on_vector):
-            rounded = ring.tile([P, PASS * PACK], BF16, name="rounded", tag="rounded", align_bytes=64)
+            if (a, b) == (PASSES - 1, PASSES - 1):
+                rounded = keep.tile([P, PASS * PACK], BF16, name="rounded_last", tag="diff0", align_bytes=64)
+            else:
+                rounded = ring.tile([P, PASS * PACK], BF16, name="rounded", tag="rounded", align_bytes=64)
             dst = rounded[:].rearrange("p (s e m i) -> p s m i e", s=2, e=2, i=PACK)
             src = wb_raw[a, b].rearrange("p i (m s e) -> p s m i e", s=2, e=2)
             nc.vector.tensor_copy(dst[:, :, :on_vector], src[:, :, :on_vector])
@@ -217,118 +215,119 @@ def tile_list_elution_balance_gap_kernel(
             h_codes[b, j] = keep.tile([P, HALF], U32, name="h_codes%d%d" % (b, j), align_bytes=64)
             h_plane[b, j] = keep.tile([P, HALF], U8, name="h_plane%d%d" % (b, j), align_bytes=64)
             pieces = range(HALF // PIECE)
+            both = keep.tile([P, HALF * PACK], BF16, name="diff%d" % b, tag="diff%d" % b, align_bytes=64)
             diff, h = [], []
             for u in pieces:
-                diff.append(ring.tile([P, PIECE * PACK], BF16, name="diff", tag="rounded", align_bytes=64))
+                diff.append(both[:, u * PIECE * PACK : (u + 1) * PIECE * PACK])
                 cols = slice(u * PIECE, (u + 1) * PIECE)
                 nc.vector.tensor_tensor(
-                    diff[u][:].rearrange("p (c e t) -> p c t e", e=2, t=PACK),
+                    diff[u].rearrange("p (c e t) -> p c t e", e=2, t=PACK),
                     exp_a[b, j][:, :, cols].rearrange("p t (c e) -> p c t e", e=2),
                     exp_b[b, j][:, :, cols].rearrange("p t (c e) -> p c t e", e=2),
                     ALU.subtract,
                 )
             for u in pieces:
                 h.append(ring.tile([P, PIECE * PACK], BF16, name="h", tag="h", align_bytes=64))
-                nc.vector.tensor_tensor(h[u][:], diff[u][:], factor[b][:].rearrange("p c t -> p (c t)"), ALU.mult)
+                nc.vector.tensor_tensor(h[u][:], diff[u], factor[:, b].rearrange("p c t -> p (c t)"), ALU.mult)
             for u in pieces:
                 cols = slice(u * PIECE, (u + 1) * PIECE)
                 nc.vector.quantize_mx(
                     out=h_codes[b, j][:, cols].bitcast(E4M3), scales=h_plane[b, j][:, cols], in_=h[u][:]
                 )
 
-        y = {}
-        for n, j in ((0, 0), (0, 1), (1, 0), (1, 1)):
-            y[n, j] = keep.tile([P, HALF], F32, name="y%d%d" % (n, j), tag="y%d%d" % (n, j))[:]
-        for n in (2, 3):
-            y[n] = keep.tile([P, S], F32, name="y%d" % n, tag="y%d" % n)[:]
-            for j in range(S // HALF):
-                y[n, j] = y[n][:, j * HALF : (j + 1) * HALF]
-        last = PAGES - 1
+        def late_features(u):
+            cols = slice((u - 2) * PIECE, (u - 1) * PIECE)
+            for b in range(PASSES):
+                nc.gpsimd.tensor_tensor(
+                    late[:, u - 2, b, :].rearrange("p (c e t) -> p c t e", e=4, t=PACK),
+                    exp_a[b, 1][:, :, cols].rearrange("p t (c e) -> p c t e", e=4),
+                    exp_b[b, 1][:, :, cols].rearrange("p t (c e) -> p c t e", e=4),
+                    ALU.subtract,
+                )
+            h = ring.tile([P, PASSES * PIECE * PACK], BF16, name="h_late", tag="rounded", align_bytes=64)
+            nc.vector.tensor_tensor(
+                h[:], late[:, u - 2].rearrange("p b c -> p (b c)"), factor[:].rearrange("p b c t -> p (b c t)"), ALU.mult
+            )
+            codes = keep.tile([P, PASSES * PIECE], U32, name="late_codes%d" % u, align_bytes=64)
+            scales = keep.tile([P, PASSES * PIECE], U8, name="late_plane%d" % u, align_bytes=64)
+            nc.vector.quantize_mx(out=codes[:].bitcast(E4M3), scales=scales[:], in_=h[:])
+            for b in range(PASSES):
+                h_piece[b, u] = (codes[:, b * PIECE : (b + 1) * PIECE], scales[:, b * PIECE : (b + 1) * PIECE])
 
-        def balance(n, j):
-            acc = y_psum.tile([P, HALF], F32, name="y_acc", tag="y_acc")
+        def product(acc, n, operands):
             for b in range(PASSES):
                 nc.tensor.matmul_mx(
-                    out=acc[:],
+                    out=acc,
                     lhsT=w8[:, b, n * P : (n + 1) * P].bitcast(E4M3),
                     lhsT_scale=plane(b, W8_AT + n * P, P),
-                    rhs=h_codes[b, j][:].bitcast(E4M3),
-                    rhs_scale=h_plane[b, j][:],
+                    rhs=operands[b][0].bitcast(E4M3),
+                    rhs_scale=operands[b][1],
                     start=(b == 0),
                     stop=(b == PASSES - 1),
                 )
-            nc.scalar.activation(y[n, j], acc[:], ACT.Copy, scale=-1.0)
-            nc.gpsimd.tensor_tensor(y[n, j], y[n, j], wgo_sb[:, j * HALF : (j + 1) * HALF], ALU.mult)
 
-        page = {}
+        page = []
+        for n in range(PAGES):
+            page.append(keep.tile([P, S], F32, name="page%d" % n))
 
-        def put(n, first, count):
-            nc.vector.tensor_copy(
-                page[n][:].indirect(place[:, first // LIST : (first + count) // LIST]),
-                y[n, first // HALF] if count == HALF else y[n],
-            )
+        def put(n, first, count, direct):
+            acc = psum.tile([P, count], F32, name="y_acc", tag="side" if first < HALF else "main")
+            if count == HALF and first == 0:
+                product(acc[:], n, [(h_codes[b, 0][:], h_plane[b, 0][:]) for b in range(PASSES)])
+            else:
+                for u in range(first // PIECE, (first + count) // PIECE):
+                    at = u * PIECE - first
+                    product(acc[:, at : at + PIECE], n, [h_piece[b, u] for b in range(PASSES)])
+            weighted = keep.tile([P, count], F32, name="weighted%d_%d" % (n, first))
+            if direct:
+                nc.vector.tensor_tensor(weighted[:], acc[:], wgo_sb[:, first : first + count], ALU.mult)
+            else:
+                y = keep.tile([P, count], F32, name="y%d_%d" % (n, first), tag="y%d_%d" % (n, first))
+                nc.scalar.copy(y[:], acc[:])
+                nc.gpsimd.tensor_tensor(weighted[:], y[:], wgo_sb[:, first : first + count], ALU.mult)
+            nc.vector.tensor_copy(page[n][:].indirect(place[:, first // LIST : (first + count) // LIST]), weighted[:])
 
-        def finish_on_tensor(n):
-            for u in range(S // HALF):
-                turned = y_psum.tile([P, HALF], F32, name="turned", tag="y_acc")
-                for c in range(HALF // P):
-                    cols = slice(u * HALF + c * P, u * HALF + (c + 1) * P)
-                    block = turned[:, c * P : (c + 1) * P]
-                    nc.tensor.matmul(block, gap[:, n, cols], ident[:], start=True, stop=False, is_transpose=True)
-                    nc.tensor.matmul(block, page[n][:, cols], ident[:], start=False, stop=True, is_transpose=True)
-                if (n, u) == (last - 1, S // HALF - 1):
-                    size_t = keep.tile([P, HALF], F32, name="size_held", tag="tail")
-                else:
-                    size_t = ring.tile([P, HALF], F32, name="size_t", tag="size_t")
-                nc.scalar.activation(size_t[:], turned[:], ACT.Abs)
-                upright = y_psum.tile([P, HALF], F32, name="upright", tag="y_acc")
-                for c in range(HALF // P):
-                    nc.tensor.transpose(upright[:, c * P : (c + 1) * P], size_t[:, c * P : (c + 1) * P], ident[:])
-                cols = slice(u * HALF, (u + 1) * HALF)
-                nc.scalar.copy(gap[:, n, cols], upright[:])
-                nc.sync.dma_start(out[n * P : (n + 1) * P, cols], gap[:, n, cols])
-
-        def finish_on_vector(n):
-            result = keep.tile([P, S], F32, name="result", tag="tail")
-            for u in range(S // PIECE):
-                cols = slice(u * PIECE, (u + 1) * PIECE)
-                nc.vector.tensor_tensor(gap[:, n, cols], gap[:, n, cols], page[n][:, cols], ALU.add)
-                nc.scalar.activation(result[:, cols], gap[:, n, cols], ACT.Abs)
-                nc.sync.dma_start(out[n * P : (n + 1) * P, cols], result[:, cols])
-
-        cation(0, 0)
-        cation(1, 0)
+        last = PAGES - 1
+        cation(0, 0, "main")
+        cation(1, 0, "side")
         quantise_wb(0, 0, P)
         quantise_wb(1, 0, P)
-        anion(0, 0)
+        anion(0, 0, "main")
+        cation(0, 1, "main")
         quantise_wb(0, 1, P)
-        quantise_wb(1, 1, P // 2)
-        anion(1, 0)
+        quantise_wb(1, 1, P)
+        anion(1, 0, "main")
+        cation(1, 1, "main")
+        anion(0, 1, "main")
         features(0, 0)
-        cation(0, 1)
-        anion(0, 1)
         features(1, 0)
-        balance(0, 0)
-        features(0, 1)
-        cation(1, 1)
-        anion(1, 1)
-        page[0] = keep.tile([P, S], F32, name="page0")
-        put(0, 0, HALF)
-        balance(1, 0)
-        features(1, 1)
-        balance(0, 1)
-        balance(1, 1)
-        for n in range(2, PAGES):
-            balance(n, 0)
-            balance(n, 1)
-        page[1] = keep.tile([P, S], F32, name="page1", tag="exp_a11")
-        put(1, 0, HALF)
-        for n in range(2):
-            put(n, HALF, HALF)
-            finish_on_tensor(n)
-        page[2] = keep.tile([P, 2 * S], F32, name="page2", tag="y11")
-        put(2, 0, S)
-        finish_on_tensor(2)
-        page[3] = keep.tile([P, 2 * S], F32, name="page3", tag="y2")
-        put(3, 0, S)
-        finish_on_vector(last)
+        for b in range(PASSES):
+            for u in range(HALF // PIECE):
+                cols = slice(u * PIECE, (u + 1) * PIECE)
+                h_piece[b, u] = (h_codes[b, 0][:, cols], h_plane[b, 0][:, cols])
+        put(0, 0, PIECE, True)
+        put(0, PIECE, PIECE, True)
+        for n in range(1, PAGES):
+            put(n, 0, HALF, n == 1)
+        anion(1, 1, "side")
+        late = keep.tile([P, 2, PASSES, PIECE * PACK], BF16, name="late", tag="diff1", align_bytes=64)
+        late_features(2)
+        late_features(3)
+        put(0, HALF, PIECE, True)
+        put(0, HALF + PIECE, PIECE, False)
+        for n in range(1, PAGES):
+            put(n, HALF, HALF, False)
+        tail_tag = "y%d_%d" % (last, HALF)
+        sums = keep.tile([P, last, S], F32, name="sums", tag=tail_tag)
+        for n in range(last):
+            for u in range(S // HALF):
+                cols = slice(u * HALF, (u + 1) * HALF)
+                nc.gpsimd.tensor_tensor(sums[:, n, cols], gap[:, n, cols], page[n][:, cols], ALU.subtract)
+                nc.scalar.activation(gap[:, n, cols], sums[:, n, cols], ACT.Abs)
+                nc.sync.dma_start(out[n * P : (n + 1) * P, cols], gap[:, n, cols])
+        result = keep.tile([P, S], F32, name="result", tag=tail_tag)
+        for u in range(S // PIECE):
+            cols = slice(u * PIECE, (u + 1) * PIECE)
+            nc.vector.tensor_tensor(gap[:, last, cols], gap[:, last, cols], page[last][:, cols], ALU.subtract)
+            nc.scalar.activation(result[:, cols], gap[:, last, cols], ACT.Abs)
+            nc.sync.dma_start(out[last * P : (last + 1) * P, cols], result[:, cols])

@@ -42,7 +42,7 @@ def tile_list_elution_balance_gap_kernel(
     with ExitStack() as ctx:
         lists = ctx.enter_context(tc.tile_pool(name="lists", bufs=1))
         keep = ctx.enter_context(tc.tile_pool(name="keep", bufs=1))
-        big = ctx.enter_context(tc.tile_pool(name="big", bufs=2))
+        big = ctx.enter_context(tc.tile_pool(name="big", bufs=1))
         ring = ctx.enter_context(tc.tile_pool(name="ring", bufs=2))
         psum = ctx.enter_context(tc.psum_pool(name="psum", bufs=4))
 
@@ -62,61 +62,53 @@ def tile_list_elution_balance_gap_kernel(
         def plane(g, first, width):
             return planes[:, g * ROW + first : g * ROW + first + width]
 
-        gain_sb = keep.tile([P, PASSES * PACK], F32, name="gain_sb")
-        nc.sync.dma_start(
-            gain_sb[:].rearrange("p (b t) -> p b t", t=PACK), gain.rearrange("(b p t) -> p b t", p=P, t=PACK)
-        )
         nc.sync.dma_start(
             tab_rows[:].bitcast(I32)[0:scale_rows, :], tab_scales.rearrange("a q t -> (a q) t").bitcast(I32)
         )
         nc.sync.dma_start(pick[:], offs)
+        nc.sync.dma_start(place[:], offs2)
         nc.sync.dma_start(
             w4_rows[:].bitcast(I32)[0:scale_rows, :], w4_scales.rearrange("a q c -> (a q) c").bitcast(I32)
         )
         nc.sync.dma_start(
             rows[:, W8_AT:].bitcast(I32)[0:scale_rows, :], w8_scales.rearrange("b q n -> (b q) n").bitcast(I32)
         )
-        tab = []
-        for a in range(PASSES):
-            tab.append(big.tile([P, T], I32, name="tab%d" % a, tag="wide", align_bytes=64))
-        nc.sync.dma_start(tab[0][:], tab_words[0].rearrange("p t i -> p (t i)").bitcast(I32))
+        gain_sb = keep.tile([P, PASSES * PACK], F32, name="gain_sb")
+        nc.sync.dma_start(
+            gain_sb[:].rearrange("p (b t) -> p b t", t=PACK), gain.rearrange("(b p t) -> p b t", p=P, t=PACK)
+        )
         w4_raw = keep.tile([P, 4 * H], U8, name="w4_raw", tag="narrow", align_bytes=64)
         nc.sync.dma_start(
             w4_raw[:].bitcast(I32).rearrange("p (a c) -> p a c", a=PASSES),
             w4_words.bitcast(I32).rearrange("a p c -> p a c"),
         )
-        nc.sync.dma_start(place[:], offs2)
-        nc.sync.dma_start(tab[1][:], tab_words[1].rearrange("p t i -> p (t i)").bitcast(I32))
+        tab = []
+        tab.append(big.tile([P, T], I32, name="tab0", tag="wide", align_bytes=64))
+        wb_raw = {}
 
-        wb_first = big.tile([P, PASSES, PACK, PASS], F32, name="wb_first", tag="wide", align_bytes=64)
-        wb_third = keep.tile([P, PACK, PASS], F32, name="wb_third", tag="narrow", align_bytes=64)
-        wb_fourth = big.tile([P, PACK, PASS], F32, name="wb_fourth", tag="wide", align_bytes=64)
-        wb_raw = {(0, 0): wb_first[:, 0], (1, 0): wb_first[:, 1], (0, 1): wb_third[:], (1, 1): wb_fourth[:]}
-        for b in range(PASSES):
-            for a in range(PASSES):
-                nc.sync.dma_start(
-                    wb_raw[a, b],
-                    wb[a * PASS : (a + 1) * PASS, b * PASS : (b + 1) * PASS].rearrange("(p i) c -> p i c", i=PACK),
-                )
-        w8 = keep.tile([P, PASSES, N], I32, name="w8", tag="narrow", align_bytes=64)
-        nc.sync.dma_start(w8[:], w8_words.rearrange("b p n i -> p b (n i)").bitcast(I32))
-        wgo_sb = big.tile([P, S], F32, name="wgo_sb", tag="wide", align_bytes=64)
-        nc.sync.dma_start(wgo_sb[:], wgo)
-        gap = big.tile([P, PAGES, S], F32, name="gap", tag="wide", align_bytes=64)
-        for n in range(PAGES):
-            nc.sync.dma_start(gap[:, n, :], x0[n * P : (n + 1) * P, :])
+        def load_wb(a, b, pool, tag):
+            wb_raw[a, b] = pool.tile([P, PACK, PASS], F32, name="wb%d%d" % (a, b), tag=tag, align_bytes=64)[:]
+            nc.sync.dma_start(
+                wb_raw[a, b],
+                wb[a * PASS : (a + 1) * PASS, b * PASS : (b + 1) * PASS].rearrange("(p i) c -> p i c", i=PACK),
+            )
+
+        load_wb(0, 0, keep, "wb00")
+        nc.sync.dma_start(tab[0][:], tab_words[0].rearrange("p t i -> p (t i)").bitcast(I32))
 
         def column(name):
             return keep.tile([P, PASSES * PACK], F32, name=name)
 
-        size, lift, drop, shift = column("size"), column("lift"), column("drop"), column("shift")
-        inner, log_gain, back, outer = column("inner"), column("log_gain"), column("back"), column("outer")
-        nc.vector.scalar_tensor_tensor(size[:], gain_sb[:], -1.0, gain_sb[:], ALU.mult, ALU.max)
-        nc.vector.tensor_scalar(lift[:], size[:], TINY, LIFT, ALU.is_lt, ALU.mult)
-        nc.vector.tensor_scalar(drop[:], size[:], HUGE, LIFT, ALU.is_le, ALU.mult)
-        nc.vector.tensor_scalar(lift[:], lift[:], 1.0, None, ALU.max)
-        nc.vector.scalar_tensor_tensor(shift[:], drop[:], DROP, lift[:], ALU.max, ALU.min)
-        nc.vector.scalar_tensor_tensor(inner[:], size[:], FLOOR, shift[:], ALU.max, ALU.mult)
+        size, tiny, lift, drop = column("size"), column("tiny"), column("lift"), column("drop")
+        floored, lifted, inner = column("floored"), column("lifted"), column("inner")
+        log_gain, back, outer = column("log_gain"), column("back"), column("outer")
+        nc.scalar.activation(size[:], gain_sb[:], ACT.Abs)
+        nc.gpsimd.tensor_scalar(tiny[:], size[:], TINY, LIFT, ALU.is_lt, ALU.mult)
+        nc.gpsimd.tensor_scalar(drop[:], size[:], HUGE, DROP, ALU.is_le, ALU.max)
+        nc.gpsimd.tensor_scalar(floored[:], size[:], FLOOR, None, ALU.max)
+        nc.gpsimd.tensor_scalar(lift[:], tiny[:], 1.0, None, ALU.max)
+        nc.gpsimd.tensor_tensor(lifted[:], floored[:], drop[:], ALU.mult)
+        nc.gpsimd.tensor_tensor(inner[:], lifted[:], lift[:], ALU.mult)
         nc.scalar.activation(log_gain[:], inner[:], ACT.Ln)
         nc.scalar.activation(back[:], log_gain[:], ACT.Exp, scale=-1.0)
         nc.vector.tensor_tensor(outer[:], gain_sb[:], back[:], ALU.mult)
@@ -127,7 +119,7 @@ def tile_list_elution_balance_gap_kernel(
                 factor[:, b], outer[:, b * PACK : (b + 1) * PACK].unsqueeze(1).to_broadcast([P, PIECE, PACK]), ACT.Copy
             )
 
-        v_rows = keep.tile([P, S], U8, name="v_rows", align_bytes=64)
+        v_rows = keep.tile([P, S], U8, name="v_rows", tag="v_rows", align_bytes=64)
         nc.vector.tensor_copy(v_rows[:], tab_rows[:].indirect(pick[:]))
         nc.vector.tensor_copy(
             rows[:, W4_AT:W8_AT].rearrange("p (b t m e) -> p b m t e", b=PASSES, t=PACK, e=16),
@@ -137,10 +129,24 @@ def tile_list_elution_balance_gap_kernel(
         moves = [(g, q) for g in range(PASSES) for q in range(QUADS)][1:]
         for g, q in moves:
             row = BLOCKS * g + 4 * q
-            queue = nc.gpsimd if (g, q) == moves[0] else nc.scalar
+            queue = nc.gpsimd if (g, q) == moves[-1] else nc.sync
             queue.dma_start(
                 plane(g, 0, ROW).bitcast(I32)[QUAD * q : QUAD * q + 4, :], rows.bitcast(I32)[row : row + 4, :]
             )
+
+        tab.append(keep.tile([P, T], I32, name="tab1", tag="v_rows", align_bytes=64))
+        nc.sync.dma_start(tab[1][:], tab_words[1].rearrange("p t i -> p (t i)").bitcast(I32))
+
+        load_wb(1, 0, keep, "narrow")
+        load_wb(0, 1, big, "wide")
+        load_wb(1, 1, keep, "v_rows")
+        w8 = keep.tile([P, PASSES, N], I32, name="w8", tag="narrow", align_bytes=64)
+        nc.sync.dma_start(w8[:], w8_words.rearrange("b p n i -> p b (n i)").bitcast(I32))
+        wgo_sb = big.tile([P, S], F32, name="wgo_sb", tag="wide", align_bytes=64)
+        nc.sync.dma_start(wgo_sb[:], wgo)
+        gap = keep.tile([P, PAGES, S], F32, name="gap", tag="v_rows", align_bytes=64)
+        for n in range(PAGES):
+            nc.sync.dma_start(gap[:, n, :], x0[n * P : (n + 1) * P, :])
 
         v = {}
 
@@ -149,14 +155,14 @@ def tile_list_elution_balance_gap_kernel(
             cols = HALF // LIST
             nc.vector.tensor_copy(v[a, j][:], tab[a][:].bitcast(U32).indirect(pick[:, j * cols : (j + 1) * cols]))
 
-        gather(0, 0)
-        gather(0, 1)
-
         w4 = keep.tile([P, 4 * H], U8, name="w4", align_bytes=64)
         nc.vector.tensor_copy(
             w4[:].bitcast(U16).rearrange("p (g t m e) -> p g m t e", g=4, t=PACK, e=8),
             w4_raw[:].bitcast(U16).rearrange("p (g m e t) -> p g m t e", g=4, t=PACK, e=8),
         )
+        gather(0, 0)
+        gather(0, 1)
+
         gather(1, 0)
         gather(1, 1)
 
@@ -181,7 +187,7 @@ def tile_list_elution_balance_gap_kernel(
                 nc.scalar.activation(exp_a[b, j][:, t, :], acc[:], ACT.Exp, bias=log_gain[:, col : col + 1])
 
         def anion(b, j, banks):
-            exp_b[b, j] = keep.tile([P, PACK, HALF], F32, name="exp_b%d%d" % (b, j))
+            exp_b[b, j] = keep.tile([P, PACK, HALF], F32, name="exp_b%d%d" % (b, j), tag="exp_b%d%d" % (b, j))
             for t in range(PACK):
                 acc = psum.tile([P, HALF], F32, name="acc", tag=banks)
                 for a in range(PASSES):
@@ -266,6 +272,7 @@ def tile_list_elution_balance_gap_kernel(
                     stop=(b == PASSES - 1),
                 )
 
+        weighted_half = {}
         page = []
         for n in range(PAGES):
             page.append(keep.tile([P, S], F32, name="page%d" % n))
@@ -278,27 +285,32 @@ def tile_list_elution_balance_gap_kernel(
                 for u in range(first // PIECE, (first + count) // PIECE):
                     at = u * PIECE - first
                     product(acc[:, at : at + PIECE], n, [h_piece[b, u] for b in range(PASSES)])
-            weighted = keep.tile([P, count], F32, name="weighted%d_%d" % (n, first))
+            half = first // HALF
+            if half not in weighted_half:
+                weighted_half[half] = keep.tile(
+                    [P, PAGES, HALF], F32, name="weighted%d" % half, tag=("exp_b00", "exp_a00")[half]
+                )
+            weighted = weighted_half[half][:, n, first % HALF : first % HALF + count]
             if direct:
-                nc.vector.tensor_tensor(weighted[:], acc[:], wgo_sb[:, first : first + count], ALU.mult)
+                nc.vector.tensor_tensor(weighted, acc[:], wgo_sb[:, first : first + count], ALU.mult)
             else:
                 y = keep.tile([P, count], F32, name="y%d_%d" % (n, first), tag="y%d_%d" % (n, first))
                 nc.scalar.copy(y[:], acc[:])
-                nc.gpsimd.tensor_tensor(weighted[:], y[:], wgo_sb[:, first : first + count], ALU.mult)
-            nc.vector.tensor_copy(page[n][:].indirect(place[:, first // LIST : (first + count) // LIST]), weighted[:])
+                nc.gpsimd.tensor_tensor(weighted, y[:], wgo_sb[:, first : first + count], ALU.mult)
+            nc.vector.tensor_copy(page[n][:].indirect(place[:, first // LIST : (first + count) // LIST]), weighted)
 
         last = PAGES - 1
-        cation(0, 0, "main")
-        cation(1, 0, "side")
         quantise_wb(0, 0, P)
+        cation(0, 0, "main")
         quantise_wb(1, 0, P)
         anion(0, 0, "main")
-        cation(0, 1, "main")
+        cation(1, 0, "side")
         quantise_wb(0, 1, P)
         quantise_wb(1, 1, P)
         anion(1, 0, "main")
-        cation(1, 1, "main")
+        cation(0, 1, "main")
         anion(0, 1, "main")
+        cation(1, 1, "main")
         features(0, 0)
         features(1, 0)
         for b in range(PASSES):

@@ -233,7 +233,10 @@ def tile_list_elution_balance_gap_kernel(
                     ALU.subtract,
                 )
             for u in pieces:
-                h.append(ring.tile([P, PIECE * PACK], BF16, name="h", tag="h", align_bytes=64))
+                if (b, u) == (PASSES - 1, HALF // PIECE - 1):
+                    h.append(keep.tile([P, PIECE * PACK], BF16, name="h_last", tag="h_last", align_bytes=64))
+                else:
+                    h.append(ring.tile([P, PIECE * PACK], BF16, name="h", tag="h", align_bytes=64))
                 nc.vector.tensor_tensor(h[u][:], diff[u], factor[:, b].rearrange("p c t -> p (c t)"), ALU.mult)
             for u in pieces:
                 cols = slice(u * PIECE, (u + 1) * PIECE)
@@ -322,7 +325,7 @@ def tile_list_elution_balance_gap_kernel(
         for n in range(1, PAGES):
             put(n, 0, HALF, n == 1)
         anion(1, 1, "side")
-        late = keep.tile([P, 2, PASSES, PIECE * PACK], BF16, name="late", tag="diff1", align_bytes=64)
+        late = keep.tile([P, 2, PASSES, PIECE * PACK], BF16, name="late", tag="h_last", align_bytes=64)
         late_features(2)
         late_features(3)
         put(0, HALF, PIECE, True)

@@ -187,7 +187,7 @@ def tile_list_elution_balance_gap_kernel(
                 nc.scalar.activation(exp_a[b, j][:, t, :], acc[:], ACT.Exp, bias=log_gain[:, col : col + 1])
 
         def anion(b, j, banks):
-            exp_b[b, j] = keep.tile([P, PACK, HALF], F32, name="exp_b%d%d" % (b, j), tag="exp_b%d%d" % (b, j))
+            exp_b[b, j] = keep.tile([P, PACK, HALF], F32, name="exp_b%d%d" % (b, j), tag="exp_b%d%d" % (b, j), align_bytes=64)
             for t in range(PACK):
                 acc = psum.tile([P, HALF], F32, name="acc", tag=banks)
                 for a in range(PASSES):
@@ -244,24 +244,29 @@ def tile_list_elution_balance_gap_kernel(
                     out=h_codes[b, j][:, cols].bitcast(E4M3), scales=h_plane[b, j][:, cols], in_=h[u][:]
                 )
 
-        def late_features(u):
-            cols = slice((u - 2) * PIECE, (u - 1) * PIECE)
-            for b in range(PASSES):
-                nc.gpsimd.tensor_tensor(
-                    late[:, u - 2, b, :].rearrange("p (c e t) -> p c t e", e=4, t=PACK),
-                    exp_a[b, 1][:, :, cols].rearrange("p t (c e) -> p c t e", e=4),
-                    exp_b[b, 1][:, :, cols].rearrange("p t (c e) -> p c t e", e=4),
-                    ALU.subtract,
+        def late_features():
+            pieces = range(HALF // PIECE)
+            late = keep.tile([P, 2, PASSES, PIECE * PACK], BF16, name="late", tag="h_last", align_bytes=64)
+            for u in pieces:
+                cols = slice(u * PIECE, (u + 1) * PIECE)
+                for b in range(PASSES):
+                    nc.gpsimd.tensor_tensor(
+                        late[:, u, b, :].rearrange("p (c e t) -> p c t e", e=4, t=PACK),
+                        exp_a[b, 1][:, :, cols].rearrange("p t (c e) -> p c t e", e=4),
+                        exp_b[b, 1][:, :, cols].rearrange("p t (c e) -> p c t e", e=4),
+                        ALU.subtract,
+                    )
+            h = keep.tile([P, 2, PASSES * PIECE * PACK], BF16, name="h_late", tag="exp_b11", align_bytes=64)
+            for u in pieces:
+                nc.vector.tensor_tensor(
+                    h[:, u], late[:, u].rearrange("p b c -> p (b c)"), factor[:].rearrange("p b c t -> p (b c t)"), ALU.mult
                 )
-            h = ring.tile([P, PASSES * PIECE * PACK], BF16, name="h_late", tag="rounded", align_bytes=64)
-            nc.vector.tensor_tensor(
-                h[:], late[:, u - 2].rearrange("p b c -> p (b c)"), factor[:].rearrange("p b c t -> p (b c t)"), ALU.mult
-            )
-            codes = keep.tile([P, PASSES * PIECE], U32, name="late_codes%d" % u, align_bytes=64)
-            scales = keep.tile([P, PASSES * PIECE], U8, name="late_plane%d" % u, align_bytes=64)
-            nc.vector.quantize_mx(out=codes[:].bitcast(E4M3), scales=scales[:], in_=h[:])
-            for b in range(PASSES):
-                h_piece[b, u] = (codes[:, b * PIECE : (b + 1) * PIECE], scales[:, b * PIECE : (b + 1) * PIECE])
+            for u in pieces:
+                codes = keep.tile([P, PASSES * PIECE], U32, name="late_codes%d" % u, align_bytes=64)
+                scales = keep.tile([P, PASSES * PIECE], U8, name="late_plane%d" % u, align_bytes=64)
+                nc.vector.quantize_mx(out=codes[:].bitcast(E4M3), scales=scales[:], in_=h[:, u])
+                for b in range(PASSES):
+                    h_piece[b, 2 + u] = (codes[:, b * PIECE : (b + 1) * PIECE], scales[:, b * PIECE : (b + 1) * PIECE])
 
         def product(acc, n, operands):
             for b in range(PASSES):
@@ -275,12 +280,12 @@ def tile_list_elution_balance_gap_kernel(
                     stop=(b == PASSES - 1),
                 )
 
-        weighted_half = {}
+        weighted = {}
         page = []
         for n in range(PAGES):
             page.append(keep.tile([P, S], F32, name="page%d" % n))
 
-        def put(n, first, count, direct):
+        def weigh(n, first, count, direct):
             acc = psum.tile([P, count], F32, name="y_acc", tag="side" if first < HALF else "main")
             if count == HALF and first == 0:
                 product(acc[:], n, [(h_codes[b, 0][:], h_plane[b, 0][:]) for b in range(PASSES)])
@@ -289,18 +294,23 @@ def tile_list_elution_balance_gap_kernel(
                     at = u * PIECE - first
                     product(acc[:, at : at + PIECE], n, [h_piece[b, u] for b in range(PASSES)])
             half = first // HALF
-            if half not in weighted_half:
-                weighted_half[half] = keep.tile(
-                    [P, PAGES, HALF], F32, name="weighted%d" % half, tag=("exp_b00", "exp_a00")[half]
+            if half not in weighted:
+                weighted[half] = keep.tile(
+                    [P, PAGES, HALF], F32, name="weighted%d" % half, tag=("exp_b00", "exp_b10")[half], align_bytes=64
                 )
-            weighted = weighted_half[half][:, n, first % HALF : first % HALF + count]
+            dst = weighted[half][:, n, first % HALF : first % HALF + count]
             if direct:
-                nc.vector.tensor_tensor(weighted, acc[:], wgo_sb[:, first : first + count], ALU.mult)
+                nc.vector.tensor_tensor(dst, acc[:], wgo_sb[:, first : first + count], ALU.mult)
             else:
                 y = keep.tile([P, count], F32, name="y%d_%d" % (n, first), tag="y%d_%d" % (n, first))
                 nc.scalar.copy(y[:], acc[:])
-                nc.gpsimd.tensor_tensor(weighted, y[:], wgo_sb[:, first : first + count], ALU.mult)
-            nc.vector.tensor_copy(page[n][:].indirect(place[:, first // LIST : (first + count) // LIST]), weighted)
+                nc.gpsimd.tensor_tensor(dst, y[:], wgo_sb[:, first : first + count], ALU.mult)
+
+        def put(n, first, count):
+            nc.vector.tensor_copy(
+                page[n][:].indirect(place[:, first // LIST : (first + count) // LIST]),
+                weighted[first // HALF][:, n, first % HALF : first % HALF + count],
+            )
 
         last = PAGES - 1
         quantise_wb(0, 0, P)
@@ -320,18 +330,22 @@ def tile_list_elution_balance_gap_kernel(
             for u in range(HALF // PIECE):
                 cols = slice(u * PIECE, (u + 1) * PIECE)
                 h_piece[b, u] = (h_codes[b, 0][:, cols], h_plane[b, 0][:, cols])
-        put(0, 0, PIECE, True)
-        put(0, PIECE, PIECE, True)
+        weigh(0, 0, PIECE, True)
+        weigh(0, PIECE, PIECE, True)
         for n in range(1, PAGES):
-            put(n, 0, HALF, n == 1)
-        anion(1, 1, "side")
-        late = keep.tile([P, 2, PASSES, PIECE * PACK], BF16, name="late", tag="h_last", align_bytes=64)
-        late_features(2)
-        late_features(3)
-        put(0, HALF, PIECE, True)
-        put(0, HALF + PIECE, PIECE, False)
+            weigh(n, 0, HALF, n == 1)
+        for n in range(PAGES):
+            put(n, 0, HALF)
+        anion(1, 1, "main")
+        late_features()
+        weigh(0, HALF, PIECE, True)
+        weigh(0, HALF + PIECE, PIECE, False)
         for n in range(1, PAGES):
-            put(n, HALF, HALF, False)
+            weigh(n, HALF, HALF, False)
+        put(0, HALF, PIECE)
+        put(0, HALF + PIECE, PIECE)
+        for n in range(1, PAGES):
+            put(n, HALF, HALF)
         tail_tag = "y%d_%d" % (last, HALF)
         sums = keep.tile([P, last, S], F32, name="sums", tag=tail_tag)
         for n in range(last):

@@ -86,14 +86,20 @@ def tile_list_elution_balance_gap_kernel(
         tab.append(big.tile([P, T], I32, name="tab0", tag="wide", align_bytes=64))
         wb_raw = {}
 
-        def load_wb(a, b, pool, tag):
-            wb_raw[a, b] = pool.tile([P, PACK, PASS], F32, name="wb%d%d" % (a, b), tag=tag, align_bytes=64)[:]
+        def take_wb(a, b, pool, tag, cuts=1):
+            raw = pool.tile([P, cuts, PACK, PASS // cuts], F32, name="wb%d%d" % (a, b), tag=tag, align_bytes=64)
+            wb_raw[a, b] = [raw[:, c] for c in range(cuts)]
+
+        def load_wb(a, b, c=0):
+            width = PASS // len(wb_raw[a, b])
+            cols = slice(b * PASS + c * width, b * PASS + (c + 1) * width)
             nc.sync.dma_start(
-                wb_raw[a, b],
-                wb[a * PASS : (a + 1) * PASS, b * PASS : (b + 1) * PASS].rearrange("(p i) c -> p i c", i=PACK),
+                wb_raw[a, b][c], wb[a * PASS : (a + 1) * PASS, cols].rearrange("(p i) c -> p i c", i=PACK)
             )
 
-        load_wb(0, 0, keep, "wb00")
+        wb_head = keep.tile([P, PACK, PASS // 2], F32, name="wb_head", align_bytes=64)
+        wb_raw[0, 0] = [wb_head[:], None]
+        load_wb(0, 0, 0)
         nc.sync.dma_start(tab[0][:], tab_words[0].rearrange("p t i -> p (t i)").bitcast(I32))
 
         def column(name):
@@ -137,9 +143,16 @@ def tile_list_elution_balance_gap_kernel(
         tab.append(keep.tile([P, T], I32, name="tab1", tag="v_rows", align_bytes=64))
         nc.sync.dma_start(tab[1][:], tab_words[1].rearrange("p t i -> p (t i)").bitcast(I32))
 
-        load_wb(1, 0, keep, "narrow")
-        load_wb(0, 1, big, "wide")
-        load_wb(1, 1, keep, "v_rows")
+        wb_next = keep.tile([P, 3, PACK, PASS // 2], F32, name="wb_next", tag="narrow", align_bytes=64)
+        wb_raw[0, 0][1] = wb_next[:, 0]
+        load_wb(0, 0, 1)
+        wb_raw[1, 0] = [wb_next[:, 1:3].rearrange("p h i c -> p (h i c)").rearrange("p (i c) -> p i c", i=PACK)]
+        load_wb(1, 0)
+        take_wb(0, 1, big, "wide")
+        load_wb(0, 1)
+        take_wb(1, 1, keep, "v_rows", 2)
+        load_wb(1, 1, 0)
+        load_wb(1, 1, 1)
         w8 = keep.tile([P, PASSES, N], I32, name="w8", tag="narrow", align_bytes=64)
         nc.sync.dma_start(w8[:], w8_words.rearrange("b p n i -> p b (n i)").bitcast(I32))
         wgo_sb = big.tile([P, S], F32, name="wgo_sb", tag="wide", align_bytes=64)
@@ -168,9 +181,10 @@ def tile_list_elution_balance_gap_kernel(
 
         exp_a, exp_b, wb_codes, wb_plane, h_codes, h_plane, h_piece = {}, {}, {}, {}, {}, {}, {}
 
-        def cation(b, j, banks):
-            exp_a[b, j] = keep.tile([P, PACK, HALF], F32, name="exp_a%d%d" % (b, j), tag="exp_a%d%d" % (b, j))
-            for t in range(PACK):
+        def cation(b, j, banks, slices=range(PACK)):
+            if (b, j) not in exp_a:
+                exp_a[b, j] = keep.tile([P, PACK, HALF], F32, name="exp_a%d%d" % (b, j), tag="exp_a%d%d" % (b, j))
+            for t in slices:
                 acc = psum.tile([P, HALF], F32, name="acc", tag=banks)
                 for a in range(PASSES):
                     first = a * H + b * PASS + t * P
@@ -203,16 +217,16 @@ def tile_list_elution_balance_gap_kernel(
                 col = b * PACK + t
                 nc.scalar.activation(exp_b[b, j][:, t, :], acc[:], ACT.Exp, bias=log_gain[:, col : col + 1])
 
-        def quantise_wb(a, b, on_vector):
+        def quantise_wb(a, b):
             if (a, b) == (PASSES - 1, PASSES - 1):
                 rounded = keep.tile([P, PASS * PACK], BF16, name="rounded_last", tag="diff0", align_bytes=64)
             else:
                 rounded = ring.tile([P, PASS * PACK], BF16, name="rounded", tag="rounded", align_bytes=64)
             dst = rounded[:].rearrange("p (s e m i) -> p s m i e", s=2, e=2, i=PACK)
-            src = wb_raw[a, b].rearrange("p i (m s e) -> p s m i e", s=2, e=2)
-            nc.vector.tensor_copy(dst[:, :, :on_vector], src[:, :, :on_vector])
-            if on_vector < P:
-                nc.scalar.copy(dst[:, :, on_vector:], src[:, :, on_vector:])
+            step = P // len(wb_raw[a, b])
+            for c, raw in enumerate(wb_raw[a, b]):
+                src = raw.rearrange("p i (m s e) -> p s m i e", s=2, e=2)
+                nc.vector.tensor_copy(dst[:, :, c * step : (c + 1) * step], src)
             wb_codes[a, b] = keep.tile([P, PASS], U32, name="wb_codes%d%d" % (a, b), align_bytes=64)
             wb_plane[a, b] = keep.tile([P, PASS], U8, name="wb_plane%d%d" % (a, b), align_bytes=64)
             nc.vector.quantize_mx(out=wb_codes[a, b][:].bitcast(E4M3), scales=wb_plane[a, b][:], in_=rounded[:])
@@ -246,21 +260,24 @@ def tile_list_elution_balance_gap_kernel(
 
         def late_features():
             pieces = range(HALF // PIECE)
-            late = keep.tile([P, 2, PASSES, PIECE * PACK], BF16, name="late", tag="h_last", align_bytes=64)
-            for u in pieces:
-                cols = slice(u * PIECE, (u + 1) * PIECE)
-                for b in range(PASSES):
+            for b in range(PASSES):
+                for g in range(2):
+                    pair = slice(2 * g, 2 * g + 2)
                     nc.gpsimd.tensor_tensor(
-                        late[:, u, b, :].rearrange("p (c e t) -> p c t e", e=4, t=PACK),
-                        exp_a[b, 1][:, :, cols].rearrange("p t (c e) -> p c t e", e=4),
-                        exp_b[b, 1][:, :, cols].rearrange("p t (c e) -> p c t e", e=4),
+                        late[:, b, g, :].rearrange("p (c i e) -> p c e i", i=4, e=2),
+                        exp_a[b, 1][:, pair, :].rearrange("p e (c i) -> p c e i", i=4),
+                        exp_b[b, 1][:, pair, :].rearrange("p e (c i) -> p c e i", i=4),
                         ALU.subtract,
                     )
             h = keep.tile([P, 2, PASSES * PIECE * PACK], BF16, name="h_late", tag="exp_b11", align_bytes=64)
             for u in pieces:
-                nc.vector.tensor_tensor(
-                    h[:, u], late[:, u].rearrange("p b c -> p (b c)"), factor[:].rearrange("p b c t -> p (b c t)"), ALU.mult
-                )
+                for b in range(PASSES):
+                    nc.vector.tensor_tensor(
+                        h[:, u].rearrange("p (b c g e) -> p b c g e", b=PASSES, g=2, e=2)[:, b],
+                        late[:, b].rearrange("p g (c e) -> p c g e", e=2)[:, u * PIECE : (u + 1) * PIECE],
+                        factor[:, b].rearrange("p c (g e) -> p c g e", e=2),
+                        ALU.mult,
+                    )
             for u in pieces:
                 codes = keep.tile([P, PASSES * PIECE], U32, name="late_codes%d" % u, align_bytes=64)
                 scales = keep.tile([P, PASSES * PIECE], U8, name="late_plane%d" % u, align_bytes=64)
@@ -302,9 +319,12 @@ def tile_list_elution_balance_gap_kernel(
             if direct:
                 nc.vector.tensor_tensor(dst, acc[:], wgo_sb[:, first : first + count], ALU.mult)
             else:
-                y = keep.tile([P, count], F32, name="y%d_%d" % (n, first), tag="y%d_%d" % (n, first))
-                nc.scalar.copy(y[:], acc[:])
-                nc.gpsimd.tensor_tensor(dst, y[:], wgo_sb[:, first : first + count], ALU.mult)
+                if first == 0:
+                    y = late[:, n // 2, n % 2, :].bitcast(F32)
+                else:
+                    y = keep.tile([P, count], F32, name="y%d_%d" % (n, first), tag="y%d_%d" % (n, first))[:]
+                nc.scalar.copy(y, acc[:])
+                nc.gpsimd.tensor_tensor(dst, y, wgo_sb[:, first : first + count], ALU.mult)
 
         def put(n, first, count):
             nc.vector.tensor_copy(
@@ -313,13 +333,13 @@ def tile_list_elution_balance_gap_kernel(
             )
 
         last = PAGES - 1
-        quantise_wb(0, 0, P)
+        quantise_wb(0, 0)
         cation(0, 0, "main")
-        quantise_wb(1, 0, P)
+        quantise_wb(1, 0)
         anion(0, 0, "main")
         cation(1, 0, "side")
-        quantise_wb(0, 1, P)
-        quantise_wb(1, 1, P)
+        quantise_wb(0, 1)
+        quantise_wb(1, 1)
         anion(1, 0, "main")
         cation(0, 1, "main")
         anion(0, 1, "main")
@@ -330,13 +350,16 @@ def tile_list_elution_balance_gap_kernel(
             for u in range(HALF // PIECE):
                 cols = slice(u * PIECE, (u + 1) * PIECE)
                 h_piece[b, u] = (h_codes[b, 0][:, cols], h_plane[b, 0][:, cols])
+        late = keep.tile([P, PASSES, 2, HALF * 2], BF16, name="late", tag="h_last", align_bytes=64)
         weigh(0, 0, PIECE, True)
         weigh(0, PIECE, PIECE, True)
         for n in range(1, PAGES):
-            weigh(n, 0, HALF, n == 1)
-        for n in range(PAGES):
+            weigh(n, 0, HALF, False)
+        put(0, 0, PIECE)
+        put(0, PIECE, PIECE)
+        for n in range(1, PAGES):
             put(n, 0, HALF)
-        anion(1, 1, "main")
+        anion(1, 1, "side")
         late_features()
         weigh(0, HALF, PIECE, True)
         weigh(0, HALF + PIECE, PIECE, False)

@@ -42,7 +42,7 @@ def tile_list_elution_balance_gap_kernel(
     with ExitStack() as ctx:
         lists = ctx.enter_context(tc.tile_pool(name="lists", bufs=1))
         keep = ctx.enter_context(tc.tile_pool(name="keep", bufs=1))
-        big = ctx.enter_context(tc.tile_pool(name="big", bufs=1))
+        big = ctx.enter_context(tc.tile_pool(name="big", bufs=2))
         ring = ctx.enter_context(tc.tile_pool(name="ring", bufs=2))
         psum = ctx.enter_context(tc.psum_pool(name="psum", bufs=4))
 
@@ -62,59 +62,66 @@ def tile_list_elution_balance_gap_kernel(
         def plane(g, first, width):
             return planes[:, g * ROW + first : g * ROW + first + width]
 
+        gain_sb = keep.tile([P, PASSES * PACK], F32, name="gain_sb")
+        nc.sync.dma_start(
+            gain_sb[:].rearrange("p (b t) -> p b t", t=PACK), gain.rearrange("(b p t) -> p b t", p=P, t=PACK)
+        )
         nc.sync.dma_start(
             tab_rows[:].bitcast(I32)[0:scale_rows, :], tab_scales.rearrange("a q t -> (a q) t").bitcast(I32)
         )
         nc.sync.dma_start(pick[:], offs)
-        nc.sync.dma_start(place[:], offs2)
         nc.sync.dma_start(
             w4_rows[:].bitcast(I32)[0:scale_rows, :], w4_scales.rearrange("a q c -> (a q) c").bitcast(I32)
         )
         nc.sync.dma_start(
             rows[:, W8_AT:].bitcast(I32)[0:scale_rows, :], w8_scales.rearrange("b q n -> (b q) n").bitcast(I32)
         )
-        gain_sb = keep.tile([P, PASSES * PACK], F32, name="gain_sb")
-        nc.sync.dma_start(
-            gain_sb[:].rearrange("p (b t) -> p b t", t=PACK), gain.rearrange("(b p t) -> p b t", p=P, t=PACK)
-        )
+        tab = []
+        for a in range(PASSES):
+            tab.append(big.tile([P, T], I32, name="tab%d" % a, tag="wide", align_bytes=64))
+        nc.sync.dma_start(tab[0][:], tab_words[0].rearrange("p t i -> p (t i)").bitcast(I32))
         w4_raw = keep.tile([P, 4 * H], U8, name="w4_raw", tag="narrow", align_bytes=64)
         nc.sync.dma_start(
             w4_raw[:].bitcast(I32).rearrange("p (a c) -> p a c", a=PASSES),
             w4_words.bitcast(I32).rearrange("a p c -> p a c"),
         )
-        tab = []
-        tab.append(big.tile([P, T], I32, name="tab0", tag="wide", align_bytes=64))
-        wb_raw = {}
+        nc.sync.dma_start(place[:], offs2)
+        nc.sync.dma_start(tab[1][:], tab_words[1].rearrange("p t i -> p (t i)").bitcast(I32))
 
-        def take_wb(a, b, pool, tag, cuts=1):
-            raw = pool.tile([P, cuts, PACK, PASS // cuts], F32, name="wb%d%d" % (a, b), tag=tag, align_bytes=64)
-            wb_raw[a, b] = [raw[:, c] for c in range(cuts)]
-
-        def load_wb(a, b, c=0):
-            width = PASS // len(wb_raw[a, b])
-            cols = slice(b * PASS + c * width, b * PASS + (c + 1) * width)
-            nc.sync.dma_start(
-                wb_raw[a, b][c], wb[a * PASS : (a + 1) * PASS, cols].rearrange("(p i) c -> p i c", i=PACK)
-            )
-
-        wb_head = keep.tile([P, PACK, PASS // 2], F32, name="wb_head", align_bytes=64)
-        wb_raw[0, 0] = [wb_head[:], None]
-        load_wb(0, 0, 0)
-        nc.sync.dma_start(tab[0][:], tab_words[0].rearrange("p t i -> p (t i)").bitcast(I32))
+        wb_first = big.tile([P, PASSES, PACK, PASS], F32, name="wb_first", tag="wide", align_bytes=64)
+        wb_third = keep.tile([P, PACK, PASS], F32, name="wb_third", tag="narrow", align_bytes=64)
+        wb_fourth = big.tile([P, 2, PACK, PASS // 2], F32, name="wb_fourth", tag="wide", align_bytes=64)
+        wb_raw = {
+            (0, 0): [wb_first[:, 0]],
+            (1, 0): [wb_first[:, 1]],
+            (0, 1): [wb_third[:]],
+            (1, 1): [wb_fourth[:, 0], wb_fourth[:, 1]],
+        }
+        for b in range(PASSES):
+            for a in range(PASSES):
+                width = PASS // len(wb_raw[a, b])
+                for c, raw in enumerate(wb_raw[a, b]):
+                    cols = slice(b * PASS + c * width, b * PASS + (c + 1) * width)
+                    nc.sync.dma_start(raw, wb[a * PASS : (a + 1) * PASS, cols].rearrange("(p i) c -> p i c", i=PACK))
+        w8 = keep.tile([P, PASSES, N], I32, name="w8", tag="narrow", align_bytes=64)
+        nc.sync.dma_start(w8[:], w8_words.rearrange("b p n i -> p b (n i)").bitcast(I32))
+        wgo_sb = big.tile([P, S], F32, name="wgo_sb", tag="wide", align_bytes=64)
+        nc.sync.dma_start(wgo_sb[:], wgo)
+        gap = big.tile([P, PAGES, S], F32, name="gap", tag="wide", align_bytes=64)
+        for n in range(PAGES):
+            nc.sync.dma_start(gap[:, n, :], x0[n * P : (n + 1) * P, :])
 
         def column(name):
             return keep.tile([P, PASSES * PACK], F32, name=name)
 
-        size, tiny, lift, drop = column("size"), column("tiny"), column("lift"), column("drop")
-        floored, lifted, inner = column("floored"), column("lifted"), column("inner")
-        log_gain, back, outer = column("log_gain"), column("back"), column("outer")
-        nc.scalar.activation(size[:], gain_sb[:], ACT.Abs)
-        nc.gpsimd.tensor_scalar(tiny[:], size[:], TINY, LIFT, ALU.is_lt, ALU.mult)
-        nc.gpsimd.tensor_scalar(drop[:], size[:], HUGE, DROP, ALU.is_le, ALU.max)
-        nc.gpsimd.tensor_scalar(floored[:], size[:], FLOOR, None, ALU.max)
-        nc.gpsimd.tensor_scalar(lift[:], tiny[:], 1.0, None, ALU.max)
-        nc.gpsimd.tensor_tensor(lifted[:], floored[:], drop[:], ALU.mult)
-        nc.gpsimd.tensor_tensor(inner[:], lifted[:], lift[:], ALU.mult)
+        size, lift, drop, shift = column("size"), column("lift"), column("drop"), column("shift")
+        inner, log_gain, back, outer = column("inner"), column("log_gain"), column("back"), column("outer")
+        nc.vector.scalar_tensor_tensor(size[:], gain_sb[:], -1.0, gain_sb[:], ALU.mult, ALU.max)
+        nc.vector.tensor_scalar(lift[:], size[:], TINY, LIFT, ALU.is_lt, ALU.mult)
+        nc.vector.tensor_scalar(drop[:], size[:], HUGE, LIFT, ALU.is_le, ALU.mult)
+        nc.vector.tensor_scalar(lift[:], lift[:], 1.0, None, ALU.max)
+        nc.vector.scalar_tensor_tensor(shift[:], drop[:], DROP, lift[:], ALU.max, ALU.min)
+        nc.vector.scalar_tensor_tensor(inner[:], size[:], FLOOR, shift[:], ALU.max, ALU.mult)
         nc.scalar.activation(log_gain[:], inner[:], ACT.Ln)
         nc.scalar.activation(back[:], log_gain[:], ACT.Exp, scale=-1.0)
         nc.vector.tensor_tensor(outer[:], gain_sb[:], back[:], ALU.mult)
@@ -125,7 +132,7 @@ def tile_list_elution_balance_gap_kernel(
                 factor[:, b], outer[:, b * PACK : (b + 1) * PACK].unsqueeze(1).to_broadcast([P, PIECE, PACK]), ACT.Copy
             )
 
-        v_rows = keep.tile([P, S], U8, name="v_rows", tag="v_rows", align_bytes=64)
+        v_rows = keep.tile([P, S], U8, name="v_rows", align_bytes=64)
         nc.vector.tensor_copy(v_rows[:], tab_rows[:].indirect(pick[:]))
         nc.vector.tensor_copy(
             rows[:, W4_AT:W8_AT].rearrange("p (b t m e) -> p b m t e", b=PASSES, t=PACK, e=16),
@@ -135,31 +142,10 @@ def tile_list_elution_balance_gap_kernel(
         moves = [(g, q) for g in range(PASSES) for q in range(QUADS)][1:]
         for g, q in moves:
             row = BLOCKS * g + 4 * q
-            queue = nc.gpsimd if (g, q) == moves[-1] else nc.sync
+            queue = nc.gpsimd if (g, q) == moves[0] else nc.scalar
             queue.dma_start(
                 plane(g, 0, ROW).bitcast(I32)[QUAD * q : QUAD * q + 4, :], rows.bitcast(I32)[row : row + 4, :]
             )
-
-        tab.append(keep.tile([P, T], I32, name="tab1", tag="v_rows", align_bytes=64))
-        nc.sync.dma_start(tab[1][:], tab_words[1].rearrange("p t i -> p (t i)").bitcast(I32))
-
-        wb_next = keep.tile([P, 3, PACK, PASS // 2], F32, name="wb_next", tag="narrow", align_bytes=64)
-        wb_raw[0, 0][1] = wb_next[:, 0]
-        load_wb(0, 0, 1)
-        wb_raw[1, 0] = [wb_next[:, 1:3].rearrange("p h i c -> p (h i c)").rearrange("p (i c) -> p i c", i=PACK)]
-        load_wb(1, 0)
-        take_wb(0, 1, big, "wide")
-        load_wb(0, 1)
-        take_wb(1, 1, keep, "v_rows", 2)
-        load_wb(1, 1, 0)
-        load_wb(1, 1, 1)
-        w8 = keep.tile([P, PASSES, N], I32, name="w8", tag="narrow", align_bytes=64)
-        nc.sync.dma_start(w8[:], w8_words.rearrange("b p n i -> p b (n i)").bitcast(I32))
-        wgo_sb = big.tile([P, S], F32, name="wgo_sb", tag="wide", align_bytes=64)
-        nc.sync.dma_start(wgo_sb[:], wgo)
-        gap = keep.tile([P, PAGES, S], F32, name="gap", tag="v_rows", align_bytes=64)
-        for n in range(PAGES):
-            nc.sync.dma_start(gap[:, n, :], x0[n * P : (n + 1) * P, :])
 
         v = {}
 
@@ -168,14 +154,14 @@ def tile_list_elution_balance_gap_kernel(
             cols = HALF // LIST
             nc.vector.tensor_copy(v[a, j][:], tab[a][:].bitcast(U32).indirect(pick[:, j * cols : (j + 1) * cols]))
 
+        gather(0, 0)
+        gather(0, 1)
+
         w4 = keep.tile([P, 4 * H], U8, name="w4", align_bytes=64)
         nc.vector.tensor_copy(
             w4[:].bitcast(U16).rearrange("p (g t m e) -> p g m t e", g=4, t=PACK, e=8),
             w4_raw[:].bitcast(U16).rearrange("p (g m e t) -> p g m t e", g=4, t=PACK, e=8),
         )
-        gather(0, 0)
-        gather(0, 1)
-
         gather(1, 0)
         gather(1, 1)
 
@@ -333,11 +319,11 @@ def tile_list_elution_balance_gap_kernel(
             )
 
         last = PAGES - 1
-        quantise_wb(0, 0)
         cation(0, 0, "main")
+        cation(1, 0, "side")
+        quantise_wb(0, 0)
         quantise_wb(1, 0)
         anion(0, 0, "main")
-        cation(1, 0, "side")
         quantise_wb(0, 1)
         quantise_wb(1, 1)
         anion(1, 0, "main")

@@ -132,6 +132,9 @@ def tile_list_elution_balance_gap_kernel(
                 factor[:, b], outer[:, b * PACK : (b + 1) * PACK].unsqueeze(1).to_broadcast([P, PIECE, PACK]), ACT.Copy
             )
 
+        exact = column("exact")
+        nc.scalar.activation(exact[:].rearrange("p (b t) -> p b t", t=PACK), factor[:, :, 0, :], ACT.Copy)
+
         v_rows = keep.tile([P, S], U8, name="v_rows", align_bytes=64)
         nc.vector.tensor_copy(v_rows[:], tab_rows[:].indirect(pick[:]))
         nc.vector.tensor_copy(
@@ -166,10 +169,11 @@ def tile_list_elution_balance_gap_kernel(
         gather(1, 1)
 
         exp_a, exp_b, wb_codes, wb_plane, h_codes, h_plane, h_piece = {}, {}, {}, {}, {}, {}, {}
+        both = {}
 
         def cation(b, j, banks, slices=range(PACK)):
-            if (b, j) not in exp_a:
-                exp_a[b, j] = keep.tile([P, PACK, HALF], F32, name="exp_a%d%d" % (b, j), tag="exp_a%d%d" % (b, j))
+            both[b, j] = keep.tile([P, 2, PACK, HALF], F32, name="exp%d%d" % (b, j), tag="exp%d%d" % (b, j), align_bytes=64)
+            exp_a[b, j] = both[b, j][:, 0]
             for t in slices:
                 acc = psum.tile([P, HALF], F32, name="acc", tag=banks)
                 for a in range(PASSES):
@@ -187,7 +191,11 @@ def tile_list_elution_balance_gap_kernel(
                 nc.scalar.activation(exp_a[b, j][:, t, :], acc[:], ACT.Exp, bias=log_gain[:, col : col + 1])
 
         def anion(b, j, banks):
-            exp_b[b, j] = keep.tile([P, PACK, HALF], F32, name="exp_b%d%d" % (b, j), tag="exp_b%d%d" % (b, j), align_bytes=64)
+            if (b, j) not in both:
+                both[b, j] = keep.tile(
+                    [P, 2, PACK, HALF], F32, name="exp%d%d" % (b, j), tag="exp%d%d" % (b, j), align_bytes=64
+                )
+            exp_b[b, j] = both[b, j][:, 1]
             for t in range(PACK):
                 acc = psum.tile([P, HALF], F32, name="acc", tag=banks)
                 for a in range(PASSES):
@@ -245,31 +253,45 @@ def tile_list_elution_balance_gap_kernel(
                 )
 
         def late_features():
-            pieces = range(HALF // PIECE)
+            third, fourth = slice(0, PIECE), slice(PIECE, HALF)
+            for b in range(PASSES):
+                for t in range(PACK):
+                    col = b * PACK + t
+                    nc.scalar.activation(
+                        both[b, 1][:, :, t, fourth], both[b, 1][:, :, t, fourth], ACT.Copy, scale=exact[:, col : col + 1]
+                    )
             for b in range(PASSES):
                 for g in range(2):
                     pair = slice(2 * g, 2 * g + 2)
                     nc.gpsimd.tensor_tensor(
-                        late[:, b, g, :].rearrange("p (c i e) -> p c e i", i=4, e=2),
-                        exp_a[b, 1][:, pair, :].rearrange("p e (c i) -> p c e i", i=4),
-                        exp_b[b, 1][:, pair, :].rearrange("p e (c i) -> p c e i", i=4),
+                        late[:, 0, b, :].rearrange("p (g c i e) -> p g c e i", g=2, i=4, e=2)[:, g],
+                        exp_a[b, 1][:, pair, third].rearrange("p e (c i) -> p c e i", i=4),
+                        exp_b[b, 1][:, pair, third].rearrange("p e (c i) -> p c e i", i=4),
                         ALU.subtract,
                     )
-            h = keep.tile([P, 2, PASSES * PIECE * PACK], BF16, name="h_late", tag="exp_b11", align_bytes=64)
-            for u in pieces:
-                for b in range(PASSES):
-                    nc.vector.tensor_tensor(
-                        h[:, u].rearrange("p (b c g e) -> p b c g e", b=PASSES, g=2, e=2)[:, b],
-                        late[:, b].rearrange("p g (c e) -> p c g e", e=2)[:, u * PIECE : (u + 1) * PIECE],
-                        factor[:, b].rearrange("p c (g e) -> p c g e", e=2),
-                        ALU.mult,
-                    )
-            for u in pieces:
+            for b in range(PASSES):
+                nc.gpsimd.tensor_tensor(
+                    late[:, 1, b, :].rearrange("p (c e t) -> p c t e", e=4, t=PACK),
+                    exp_a[b, 1][:, :, fourth].rearrange("p t (c e) -> p c t e", e=4),
+                    exp_b[b, 1][:, :, fourth].rearrange("p t (c e) -> p c t e", e=4),
+                    ALU.subtract,
+                )
+            h = keep.tile([P, PASSES, PIECE * PACK], BF16, name="h_late", tag="exp11", align_bytes=64)
+            for b in range(PASSES):
+                nc.vector.tensor_tensor(
+                    h[:, b].rearrange("p (c g e) -> p c g e", g=2, e=2),
+                    late[:, 0, b, :].rearrange("p (g c e) -> p c g e", g=2, e=2),
+                    factor[:, b].rearrange("p c (g e) -> p c g e", e=2),
+                    ALU.mult,
+                )
+            for u, rounded in ((3, late[:, 1]), (2, h[:])):
                 codes = keep.tile([P, PASSES * PIECE], U32, name="late_codes%d" % u, align_bytes=64)
                 scales = keep.tile([P, PASSES * PIECE], U8, name="late_plane%d" % u, align_bytes=64)
-                nc.vector.quantize_mx(out=codes[:].bitcast(E4M3), scales=scales[:], in_=h[:, u])
+                nc.vector.quantize_mx(
+                    out=codes[:].bitcast(E4M3), scales=scales[:], in_=rounded.rearrange("p b c -> p (b c)")
+                )
                 for b in range(PASSES):
-                    h_piece[b, 2 + u] = (codes[:, b * PIECE : (b + 1) * PIECE], scales[:, b * PIECE : (b + 1) * PIECE])
+                    h_piece[b, u] = (codes[:, b * PIECE : (b + 1) * PIECE], scales[:, b * PIECE : (b + 1) * PIECE])
 
         def product(acc, n, operands):
             for b in range(PASSES):
@@ -293,13 +315,13 @@ def tile_list_elution_balance_gap_kernel(
             if count == HALF and first == 0:
                 product(acc[:], n, [(h_codes[b, 0][:], h_plane[b, 0][:]) for b in range(PASSES)])
             else:
-                for u in range(first // PIECE, (first + count) // PIECE):
+                for u in reversed(range(first // PIECE, (first + count) // PIECE)):
                     at = u * PIECE - first
                     product(acc[:, at : at + PIECE], n, [h_piece[b, u] for b in range(PASSES)])
             half = first // HALF
             if half not in weighted:
                 weighted[half] = keep.tile(
-                    [P, PAGES, HALF], F32, name="weighted%d" % half, tag=("exp_b00", "exp_b10")[half], align_bytes=64
+                    [P, PAGES, HALF], F32, name="weighted%d" % half, tag=("exp00", "exp10")[half], align_bytes=64
                 )
             dst = weighted[half][:, n, first % HALF : first % HALF + count]
             if direct:
@@ -347,19 +369,19 @@ def tile_list_elution_balance_gap_kernel(
             put(n, 0, HALF)
         anion(1, 1, "side")
         late_features()
-        weigh(0, HALF, PIECE, True)
-        weigh(0, HALF + PIECE, PIECE, False)
+        weigh(0, HALF + PIECE, PIECE, True)
+        weigh(0, HALF, PIECE, False)
         for n in range(1, PAGES):
             weigh(n, HALF, HALF, False)
-        put(0, HALF, PIECE)
         put(0, HALF + PIECE, PIECE)
+        put(0, HALF, PIECE)
         for n in range(1, PAGES):
             put(n, HALF, HALF)
         tail_tag = "y%d_%d" % (last, HALF)
         sums = keep.tile([P, last, S], F32, name="sums", tag=tail_tag)
         for n in range(last):
-            for u in range(S // HALF):
-                cols = slice(u * HALF, (u + 1) * HALF)
+            cuts = (0, HALF, HALF + PIECE, S) if n == last - 1 else (0, S)
+            for cols in map(slice, cuts, cuts[1:]):
                 nc.gpsimd.tensor_tensor(sums[:, n, cols], gap[:, n, cols], page[n][:, cols], ALU.subtract)
                 nc.scalar.activation(gap[:, n, cols], sums[:, n, cols], ACT.Abs)
                 nc.sync.dma_start(out[n * P : (n + 1) * P, cols], gap[:, n, cols])

@@ -172,7 +172,10 @@ def tile_list_elution_balance_gap_kernel(
         both = {}
 
         def cation(b, j, banks, slices=range(PACK)):
-            both[b, j] = keep.tile([P, 2, PACK, HALF], F32, name="exp%d%d" % (b, j), tag="exp%d%d" % (b, j), align_bytes=64)
+            if (b, j) not in both:
+                both[b, j] = keep.tile(
+                    [P, 2, PACK, HALF], F32, name="exp%d%d" % (b, j), tag="exp%d%d" % (b, j), align_bytes=64
+                )
             exp_a[b, j] = both[b, j][:, 0]
             for t in slices:
                 acc = psum.tile([P, HALF], F32, name="acc", tag=banks)
@@ -327,8 +330,8 @@ def tile_list_elution_balance_gap_kernel(
             if direct:
                 nc.vector.tensor_tensor(dst, acc[:], wgo_sb[:, first : first + count], ALU.mult)
             else:
-                if first == 0:
-                    y = late[:, n // 2, n % 2, :].bitcast(F32)
+                if first < HALF:
+                    y = late[:, n // 2, n % 2, 2 * first :].bitcast(F32)
                 else:
                     y = keep.tile([P, count], F32, name="y%d_%d" % (n, first), tag="y%d_%d" % (n, first))[:]
                 nc.scalar.copy(y, acc[:])
@@ -351,7 +354,7 @@ def tile_list_elution_balance_gap_kernel(
         anion(1, 0, "main")
         cation(0, 1, "main")
         anion(0, 1, "main")
-        cation(1, 1, "main")
+        cation(1, 1, "main", range(2))
         features(0, 0)
         features(1, 0)
         for b in range(PASSES):
@@ -367,6 +370,7 @@ def tile_list_elution_balance_gap_kernel(
         put(0, PIECE, PIECE)
         for n in range(1, PAGES):
             put(n, 0, HALF)
+        cation(1, 1, "side", range(2, PACK))
         anion(1, 1, "side")
         late_features()
         weigh(0, HALF + PIECE, PIECE, True)

@@ -244,7 +244,7 @@ def tile_list_elution_balance_gap_kernel(
                     ALU.subtract,
                 )
             for u in pieces:
-                if (b, u) == (PASSES - 1, HALF // PIECE - 1):
+                if (b, u) == (PASSES - 1, 0):
                     h.append(keep.tile([P, PIECE * PACK], BF16, name="h_last", tag="h_last", align_bytes=64))
                 else:
                     h.append(ring.tile([P, PIECE * PACK], BF16, name="h", tag="h", align_bytes=64))
@@ -335,7 +335,15 @@ def tile_list_elution_balance_gap_kernel(
                 else:
                     y = keep.tile([P, count], F32, name="y%d_%d" % (n, first), tag="y%d_%d" % (n, first))[:]
                 nc.scalar.copy(y, acc[:])
-                nc.gpsimd.tensor_tensor(dst, y, wgo_sb[:, first : first + count], ALU.mult)
+                if first >= HALF or n == 1:
+                    nc.gpsimd.tensor_tensor(dst, y, wgo_sb[:, first : first + count], ALU.mult)
+                elif n == PAGES - 1:
+                    nc.gpsimd.tensor_tensor(
+                        weighted[0][:, 2:],
+                        late[:, 1].bitcast(F32),
+                        wgo_sb[:, :HALF].unsqueeze(1).to_broadcast([P, 2, HALF]),
+                        ALU.mult,
+                    )
 
         def put(n, first, count):
             nc.vector.tensor_copy(

@@ -279,6 +279,15 @@ def tile_list_elution_balance_gap_kernel(
                     exp_b[b, 1][:, :, fourth].rearrange("p t (c e) -> p c t e", e=4),
                     ALU.subtract,
                 )
+
+        def quantise_late(u, rounded):
+            codes = keep.tile([P, PASSES * PIECE], U32, name="late_codes%d" % u, align_bytes=64)
+            scales = keep.tile([P, PASSES * PIECE], U8, name="late_plane%d" % u, align_bytes=64)
+            nc.vector.quantize_mx(out=codes[:].bitcast(E4M3), scales=scales[:], in_=rounded.rearrange("p b c -> p (b c)"))
+            for b in range(PASSES):
+                h_piece[b, u] = (codes[:, b * PIECE : (b + 1) * PIECE], scales[:, b * PIECE : (b + 1) * PIECE])
+
+        def sign_late():
             h = keep.tile([P, PASSES, PIECE * PACK], BF16, name="h_late", tag="exp11", align_bytes=64)
             for b in range(PASSES):
                 nc.vector.tensor_tensor(
@@ -287,14 +296,7 @@ def tile_list_elution_balance_gap_kernel(
                     factor[:, b].rearrange("p c (g e) -> p c g e", e=2),
                     ALU.mult,
                 )
-            for u, rounded in ((3, late[:, 1]), (2, h[:])):
-                codes = keep.tile([P, PASSES * PIECE], U32, name="late_codes%d" % u, align_bytes=64)
-                scales = keep.tile([P, PASSES * PIECE], U8, name="late_plane%d" % u, align_bytes=64)
-                nc.vector.quantize_mx(
-                    out=codes[:].bitcast(E4M3), scales=scales[:], in_=rounded.rearrange("p b c -> p (b c)")
-                )
-                for b in range(PASSES):
-                    h_piece[b, u] = (codes[:, b * PIECE : (b + 1) * PIECE], scales[:, b * PIECE : (b + 1) * PIECE])
+            return h
 
         def product(acc, n, operands):
             for b in range(PASSES):
@@ -333,7 +335,8 @@ def tile_list_elution_balance_gap_kernel(
                 if first < HALF:
                     y = late[:, n // 2, n % 2, 2 * first :].bitcast(F32)
                 else:
-                    y = keep.tile([P, count], F32, name="y%d_%d" % (n, first), tag="y%d_%d" % (n, first))[:]
+                    tag = "exp11" if (n, first) == (1, HALF + PIECE) else "y%d_%d" % (n, first)
+                    y = keep.tile([P, count], F32, name="y%d_%d" % (n, first), tag=tag, align_bytes=64)[:]
                 nc.scalar.copy(y, acc[:])
                 if first >= HALF or n == 1:
                     nc.gpsimd.tensor_tensor(dst, y, wgo_sb[:, first : first + count], ALU.mult)
@@ -381,25 +384,32 @@ def tile_list_elution_balance_gap_kernel(
         cation(1, 1, "side", range(2, PACK))
         anion(1, 1, "side")
         late_features()
+        quantise_late(3, late[:, 1])
+        h_third = sign_late()
         weigh(0, HALF + PIECE, PIECE, True)
-        weigh(0, HALF, PIECE, False)
-        for n in range(1, PAGES):
+        quantise_late(2, h_third[:])
+        weigh(1, HALF + PIECE, PIECE, False)
+        for n in range(2):
+            weigh(n, HALF, PIECE, False)
+        for n in range(2, PAGES):
             weigh(n, HALF, HALF, False)
-        put(0, HALF + PIECE, PIECE)
-        put(0, HALF, PIECE)
-        for n in range(1, PAGES):
+        for first in (HALF + PIECE, HALF):
+            for n in range(2):
+                put(n, first, PIECE)
+        for n in range(2, PAGES):
             put(n, HALF, HALF)
         tail_tag = "y%d_%d" % (last, HALF)
-        sums = keep.tile([P, last, S], F32, name="sums", tag=tail_tag)
+        sums = keep.tile([P, last, S], F32, name="sums", tag=tail_tag, align_bytes=64)
         for n in range(last):
             cuts = (0, HALF, HALF + PIECE, S) if n == last - 1 else (0, S)
             for cols in map(slice, cuts, cuts[1:]):
                 nc.gpsimd.tensor_tensor(sums[:, n, cols], gap[:, n, cols], page[n][:, cols], ALU.subtract)
                 nc.scalar.activation(gap[:, n, cols], sums[:, n, cols], ACT.Abs)
                 nc.sync.dma_start(out[n * P : (n + 1) * P, cols], gap[:, n, cols])
-        result = keep.tile([P, S], F32, name="result", tag=tail_tag)
+        result = keep.tile([P, S], F32, name="result", tag=tail_tag, align_bytes=64)
         for u in range(S // PIECE):
             cols = slice(u * PIECE, (u + 1) * PIECE)
             nc.vector.tensor_tensor(gap[:, last, cols], gap[:, last, cols], page[last][:, cols], ALU.subtract)
             nc.scalar.activation(result[:, cols], gap[:, last, cols], ACT.Abs)
-            nc.sync.dma_start(out[last * P : (last + 1) * P, cols], result[:, cols])
+            queue = nc.scalar if u == S // PIECE - 1 else nc.sync
+            queue.dma_start(out[last * P : (last + 1) * P, cols], result[:, cols])

from contextlib import ExitStack

import concourse.mybir as mybir

K, T, S, H, N = 1024, 4096, 1024, 1024, 512
FLOPS = 2 * (2 * K * H * S + H * N * S)

F32 = mybir.dt.float32
BF16 = mybir.dt.bfloat16
I32 = mybir.dt.int32
U32 = mybir.dt.uint32
U16 = mybir.dt.uint16
U8 = mybir.dt.uint8
E4M3 = mybir.dt.float8_e4m3fn_x4
E2M1 = mybir.dt.float4_e2m1fn_x4
ALU = mybir.AluOpType
ACT = mybir.ActivationFunctionType

P = 128
PACK = 4
PASS = P * PACK
PASSES = 2
QUADS = 4
QUAD = P // QUADS
BLOCKS = PASS // 32
HALF = 512
PIECE = 256
LIST = 16
PAGES = N // P

V_AT, W4_AT, W8_AT, ROW = 0, S, S + H, S + H + N

TINY, LIFT = 2.0**-50, 2.0**90
HUGE, DROP = 2.0**50, 2.0**-70
FLOOR = 2.0**-126


def tile_list_elution_balance_gap_kernel(
    tc, tab_words, tab_scales, offs, w4_words, w4_scales, wb, gain, w8_words, w8_scales, offs2, wgo, x0, out
):
    nc = tc.nc
    with ExitStack() as ctx:
        lists = ctx.enter_context(tc.tile_pool(name="lists", bufs=1))
        keep = ctx.enter_context(tc.tile_pool(name="keep", bufs=1))
        big = ctx.enter_context(tc.tile_pool(name="big", bufs=2))
        ring = ctx.enter_context(tc.tile_pool(name="ring", bufs=2))
        psum = ctx.enter_context(tc.psum_pool(name="psum", bufs=4))

        pick = lists.tile([P, S // LIST], U16, name="pick")
        place = lists.tile([P, S // LIST], U16, name="place")

        scale_rows = PASSES * BLOCKS
        tab_rows = keep.tile([P, T], U8, name="tab_rows", align_bytes=64)
        w4_rows = keep.tile([P, H], U8, name="w4_rows", align_bytes=64)
        planes = keep.tile([P, PASSES * ROW], U8, name="planes", align_bytes=64)
        rows = planes[:, :ROW]
        for loaded in (tab_rows[:], w4_rows[:], rows[:, W8_AT:]):
            nc.vector.memset(loaded.bitcast(I32)[scale_rows : P // 2, :], 0)
            nc.vector.memset(loaded.bitcast(I32)[P // 2 : P, :], 0)
        nc.gpsimd.memset(planes[:, ROW:].bitcast(I32), 0)

        def plane(g, first, width):
            return planes[:, g * ROW + first : g * ROW + first + width]

        gain_sb = keep.tile([P, PASSES * PACK], F32, name="gain_sb")
        nc.sync.dma_start(
            gain_sb[:].rearrange("p (b t) -> p b t", t=PACK), gain.rearrange("(b p t) -> p b t", p=P, t=PACK)
        )
        nc.sync.dma_start(
            tab_rows[:].bitcast(I32)[0:scale_rows, :], tab_scales.rearrange("a q t -> (a q) t").bitcast(I32)
        )
        nc.sync.dma_start(pick[:], offs)
        nc.sync.dma_start(
            w4_rows[:].bitcast(I32)[0:scale_rows, :], w4_scales.rearrange("a q c -> (a q) c").bitcast(I32)
        )
        nc.sync.dma_start(
            rows[:, W8_AT:].bitcast(I32)[0:scale_rows, :], w8_scales.rearrange("b q n -> (b q) n").bitcast(I32)
        )
        tab = []
        for a in range(PASSES):
            tab.append(big.tile([P, T], I32, name="tab%d" % a, tag="wide", align_bytes=64))
        nc.sync.dma_start(tab[0][:], tab_words[0].rearrange("p t i -> p (t i)").bitcast(I32))
        w4_raw = keep.tile([P, 4 * H], U8, name="w4_raw", tag="narrow", align_bytes=64)
        nc.sync.dma_start(
            w4_raw[:].bitcast(I32).rearrange("p (a c) -> p a c", a=PASSES),
            w4_words.bitcast(I32).rearrange("a p c -> p a c"),
        )
        nc.sync.dma_start(place[:], offs2)
        nc.sync.dma_start(tab[1][:], tab_words[1].rearrange("p t i -> p (t i)").bitcast(I32))

        wb_first = big.tile([P, PASSES, PACK, PASS], F32, name="wb_first", tag="wide", align_bytes=64)
        wb_third = keep.tile([P, PACK, PASS], F32, name="wb_third", tag="narrow", align_bytes=64)
        wb_fourth = big.tile([P, 2, PACK, PASS // 2], F32, name="wb_fourth", tag="wide", align_bytes=64)
        wb_raw = {
            (0, 0): [wb_first[:, 0]],
            (1, 0): [wb_first[:, 1]],
            (0, 1): [wb_third[:]],
            (1, 1): [wb_fourth[:, 0], wb_fourth[:, 1]],
        }
        for b in range(PASSES):
            for a in range(PASSES):
                width = PASS // len(wb_raw[a, b])
                for c, raw in enumerate(wb_raw[a, b]):
                    cols = slice(b * PASS + c * width, b * PASS + (c + 1) * width)
                    nc.sync.dma_start(raw, wb[a * PASS : (a + 1) * PASS, cols].rearrange("(p i) c -> p i c", i=PACK))
        w8 = keep.tile([P, PASSES, N], I32, name="w8", tag="narrow", align_bytes=64)
        nc.sync.dma_start(w8[:], w8_words.rearrange("b p n i -> p b (n i)").bitcast(I32))
        wgo_sb = big.tile([P, S], F32, name="wgo_sb", tag="wide", align_bytes=64)
        nc.sync.dma_start(wgo_sb[:], wgo)
        gap = big.tile([P, PAGES, S], F32, name="gap", tag="wide", align_bytes=64)
        for n in range(PAGES):
            nc.sync.dma_start(gap[:, n, :], x0[n * P : (n + 1) * P, :])

        def column(name):
            return keep.tile([P, PASSES * PACK], F32, name=name)

        size, lift, drop, shift = column("size"), column("lift"), column("drop"), column("shift")
        inner, log_gain, back, outer = column("inner"), column("log_gain"), column("back"), column("outer")
        nc.vector.scalar_tensor_tensor(size[:], gain_sb[:], -1.0, gain_sb[:], ALU.mult, ALU.max)
        nc.vector.tensor_scalar(lift[:], size[:], TINY, LIFT, ALU.is_lt, ALU.mult)
        nc.vector.tensor_scalar(drop[:], size[:], HUGE, LIFT, ALU.is_le, ALU.mult)
        nc.vector.tensor_scalar(lift[:], lift[:], 1.0, None, ALU.max)
        nc.vector.scalar_tensor_tensor(shift[:], drop[:], DROP, lift[:], ALU.max, ALU.min)
        nc.vector.scalar_tensor_tensor(inner[:], size[:], FLOOR, shift[:], ALU.max, ALU.mult)
        nc.scalar.activation(log_gain[:], inner[:], ACT.Ln)
        nc.scalar.activation(back[:], log_gain[:], ACT.Exp, scale=-1.0)
        nc.vector.tensor_tensor(outer[:], gain_sb[:], back[:], ALU.mult)

        factor = keep.tile([P, PASSES, PIECE, PACK], BF16, name="factor", align_bytes=64)
        for b in range(PASSES):
            nc.scalar.activation(
                factor[:, b], outer[:, b * PACK : (b + 1) * PACK].unsqueeze(1).to_broadcast([P, PIECE, PACK]), ACT.Copy
            )

        exact = column("exact")
        nc.scalar.activation(exact[:].rearrange("p (b t) -> p b t", t=PACK), factor[:, :, 0, :], ACT.Copy)

        v_rows = keep.tile([P, S], U8, name="v_rows", align_bytes=64)
        nc.vector.tensor_copy(v_rows[:], tab_rows[:].indirect(pick[:]))
        nc.vector.tensor_copy(
            rows[:, W4_AT:W8_AT].rearrange("p (b t m e) -> p b m t e", b=PASSES, t=PACK, e=16),
            w4_rows[:].rearrange("p (b m e t) -> p b m t e", b=PASSES, t=PACK, e=16),
        )
        nc.vector.tensor_copy(rows[:, V_AT:W4_AT].bitcast(I32), v_rows[:].bitcast(I32))
        moves = [(g, q) for g in range(PASSES) for q in range(QUADS)][1:]
        for g, q in moves:
            row = BLOCKS * g + 4 * q
            queue = nc.gpsimd if (g, q) == moves[0] else nc.scalar
            queue.dma_start(
                plane(g, 0, ROW).bitcast(I32)[QUAD * q : QUAD * q + 4, :], rows.bitcast(I32)[row : row + 4, :]
            )

        v = {}

        def gather(a, j):
            v[a, j] = keep.tile([P, HALF], U32, name="v%d%d" % (a, j), align_bytes=64)
            cols = HALF // LIST
            nc.vector.tensor_copy(v[a, j][:], tab[a][:].bitcast(U32).indirect(pick[:, j * cols : (j + 1) * cols]))

        gather(0, 0)
        gather(0, 1)

        w4 = keep.tile([P, 4 * H], U8, name="w4", align_bytes=64)
        nc.vector.tensor_copy(
            w4[:].bitcast(U16).rearrange("p (g t m e) -> p g m t e", g=4, t=PACK, e=8),
            w4_raw[:].bitcast(U16).rearrange("p (g m e t) -> p g m t e", g=4, t=PACK, e=8),
        )
        gather(1, 0)
        gather(1, 1)

        exp_a, exp_b, wb_codes, wb_plane, h_codes, h_plane, h_piece = {}, {}, {}, {}, {}, {}, {}
        both = {}

        def cation(b, j, banks, slices=range(PACK)):
            if (b, j) not in both:
                both[b, j] = keep.tile(
                    [P, 2, PACK, HALF], F32, name="exp%d%d" % (b, j), tag="exp%d%d" % (b, j), align_bytes=64
                )
            exp_a[b, j] = both[b, j][:, 0]
            for t in slices:
                acc = psum.tile([P, HALF], F32, name="acc", tag=banks)
                for a in range(PASSES):
                    first = a * H + b * PASS + t * P
                    nc.tensor.matmul_mx(
                        out=acc[:],
                        lhsT=w4[:, 2 * first : 2 * (first + P)].bitcast(E2M1),
                        lhsT_scale=plane(a, W4_AT + b * PASS + t * P, P),
                        rhs=v[a, j][:].bitcast(E4M3),
                        rhs_scale=plane(a, V_AT + j * HALF, HALF),
                        start=(a == 0),
                        stop=(a == PASSES - 1),
                    )
                col = b * PACK + t
                nc.scalar.activation(exp_a[b, j][:, t, :], acc[:], ACT.Exp, bias=log_gain[:, col : col + 1])

        def anion(b, j, banks):
            if (b, j) not in both:
                both[b, j] = keep.tile(
                    [P, 2, PACK, HALF], F32, name="exp%d%d" % (b, j), tag="exp%d%d" % (b, j), align_bytes=64
                )
            exp_b[b, j] = both[b, j][:, 1]
            for t in range(PACK):
                acc = psum.tile([P, HALF], F32, name="acc", tag=banks)
                for a in range(PASSES):
                    nc.tensor.matmul_mx(
                        out=acc[:],
                        lhsT=wb_codes[a, b][:, t * P : (t + 1) * P].bitcast(E4M3),
                        lhsT_scale=wb_plane[a, b][:, t * P : (t + 1) * P],
                        rhs=v[a, j][:].bitcast(E4M3),
                        rhs_scale=plane(a, V_AT + j * HALF, HALF),
                        start=(a == 0),
                        stop=(a == PASSES - 1),
                    )
                col = b * PACK + t
                nc.scalar.activation(exp_b[b, j][:, t, :], acc[:], ACT.Exp, bias=log_gain[:, col : col + 1])

        def quantise_wb(a, b):
            if (a, b) == (PASSES - 1, PASSES - 1):
                rounded = keep.tile([P, PASS * PACK], BF16, name="rounded_last", tag="diff0", align_bytes=64)
            else:
                rounded = ring.tile([P, PASS * PACK], BF16, name="rounded", tag="rounded", align_bytes=64)
            dst = rounded[:].rearrange("p (s e m i) -> p s m i e", s=2, e=2, i=PACK)
            step = P // len(wb_raw[a, b])
            for c, raw in enumerate(wb_raw[a, b]):
                src = raw.rearrange("p i (m s e) -> p s m i e", s=2, e=2)
                nc.vector.tensor_copy(dst[:, :, c * step : (c + 1) * step], src)
            wb_codes[a, b] = keep.tile([P, PASS], U32, name="wb_codes%d%d" % (a, b), align_bytes=64)
            wb_plane[a, b] = keep.tile([P, PASS], U8, name="wb_plane%d%d" % (a, b), align_bytes=64)
            nc.vector.quantize_mx(out=wb_codes[a, b][:].bitcast(E4M3), scales=wb_plane[a, b][:], in_=rounded[:])

        def features(b, j):
            h_codes[b, j] = keep.tile([P, HALF], U32, name="h_codes%d%d" % (b, j), align_bytes=64)
            h_plane[b, j] = keep.tile([P, HALF], U8, name="h_plane%d%d" % (b, j), align_bytes=64)
            pieces = range(HALF // PIECE)
            both = keep.tile([P, HALF * PACK], BF16, name="diff%d" % b, tag="diff%d" % b, align_bytes=64)
            diff, h = [], []
            for u in pieces:
                diff.append(both[:, u * PIECE * PACK : (u + 1) * PIECE * PACK])
                cols = slice(u * PIECE, (u + 1) * PIECE)
                nc.vector.tensor_tensor(
                    diff[u].rearrange("p (c e t) -> p c t e", e=2, t=PACK),
                    exp_a[b, j][:, :, cols].rearrange("p t (c e) -> p c t e", e=2),
                    exp_b[b, j][:, :, cols].rearrange("p t (c e) -> p c t e", e=2),
                    ALU.subtract,
                )
            for u in pieces:
                if (b, u) == (PASSES - 1, 0):
                    h.append(keep.tile([P, PIECE * PACK], BF16, name="h_last", tag="h_last", align_bytes=64))
                else:
                    h.append(ring.tile([P, PIECE * PACK], BF16, name="h", tag="h", align_bytes=64))
                nc.vector.tensor_tensor(h[u][:], diff[u], factor[:, b].rearrange("p c t -> p (c t)"), ALU.mult)
            for u in pieces:
                cols = slice(u * PIECE, (u + 1) * PIECE)
                nc.vector.quantize_mx(
                    out=h_codes[b, j][:, cols].bitcast(E4M3), scales=h_plane[b, j][:, cols], in_=h[u][:]
                )

        def late_features():
            third, fourth = slice(0, PIECE), slice(PIECE, HALF)
            for b in range(PASSES):
                for t in range(PACK):
                    col = b * PACK + t
                    nc.scalar.activation(
                        both[b, 1][:, :, t, fourth], both[b, 1][:, :, t, fourth], ACT.Copy, scale=exact[:, col : col + 1]
                    )
            for b in range(PASSES):
                for g in range(2):
                    pair = slice(2 * g, 2 * g + 2)
                    nc.gpsimd.tensor_tensor(
                        late[:, 0, b, :].rearrange("p (g c i e) -> p g c e i", g=2, i=4, e=2)[:, g],
                        exp_a[b, 1][:, pair, third].rearrange("p e (c i) -> p c e i", i=4),
                        exp_b[b, 1][:, pair, third].rearrange("p e (c i) -> p c e i", i=4),
                        ALU.subtract,
                    )
            for b in range(PASSES):
                nc.gpsimd.tensor_tensor(
                    late[:, 1, b, :].rearrange("p (c e t) -> p c t e", e=4, t=PACK),
                    exp_a[b, 1][:, :, fourth].rearrange("p t (c e) -> p c t e", e=4),
                    exp_b[b, 1][:, :, fourth].rearrange("p t (c e) -> p c t e", e=4),
                    ALU.subtract,
                )

        def quantise_late(u, rounded):
            codes = keep.tile([P, PASSES * PIECE], U32, name="late_codes%d" % u, align_bytes=64)
            scales = keep.tile([P, PASSES * PIECE], U8, name="late_plane%d" % u, align_bytes=64)
            nc.vector.quantize_mx(out=codes[:].bitcast(E4M3), scales=scales[:], in_=rounded.rearrange("p b c -> p (b c)"))
            for b in range(PASSES):
                h_piece[b, u] = (codes[:, b * PIECE : (b + 1) * PIECE], scales[:, b * PIECE : (b + 1) * PIECE])

        def sign_late():
            h = keep.tile([P, PASSES, PIECE * PACK], BF16, name="h_late", tag="exp11", align_bytes=64)
            for b in range(PASSES):
                nc.vector.tensor_tensor(
                    h[:, b].rearrange("p (c g e) -> p c g e", g=2, e=2),
                    late[:, 0, b, :].rearrange("p (g c e) -> p c g e", g=2, e=2),
                    factor[:, b].rearrange("p c (g e) -> p c g e", e=2),
                    ALU.mult,
                )
            return h

        def product(acc, n, operands):
            for b in range(PASSES):
                nc.tensor.matmul_mx(
                    out=acc,
                    lhsT=w8[:, b, n * P : (n + 1) * P].bitcast(E4M3),
                    lhsT_scale=plane(b, W8_AT + n * P, P),
                    rhs=operands[b][0].bitcast(E4M3),
                    rhs_scale=operands[b][1],
                    start=(b == 0),
                    stop=(b == PASSES - 1),
                )

        weighted = {}
        page = []
        for n in range(PAGES):
            page.append(keep.tile([P, S], F32, name="page%d" % n))

        def weigh(n, first, count, direct):
            acc = psum.tile([P, count], F32, name="y_acc", tag="side" if first < HALF else "main")
            if count == HALF and first == 0:
                product(acc[:], n, [(h_codes[b, 0][:], h_plane[b, 0][:]) for b in range(PASSES)])
            else:
                for u in reversed(range(first // PIECE, (first + count) // PIECE)):
                    at = u * PIECE - first
                    product(acc[:, at : at + PIECE], n, [h_piece[b, u] for b in range(PASSES)])
            half = first // HALF
            if half not in weighted:
                weighted[half] = keep.tile(
                    [P, PAGES, HALF], F32, name="weighted%d" % half, tag=("exp00", "exp10")[half], align_bytes=64
                )
            dst = weighted[half][:, n, first % HALF : first % HALF + count]
            if direct:
                nc.vector.tensor_tensor(dst, acc[:], wgo_sb[:, first : first + count], ALU.mult)
            else:
                if first < HALF:
                    y = late[:, n // 2, n % 2, 2 * first :].bitcast(F32)
                else:
                    tag = "exp11" if (n, first) == (1, HALF + PIECE) else "y%d_%d" % (n, first)
                    y = keep.tile([P, count], F32, name="y%d_%d" % (n, first), tag=tag, align_bytes=64)[:]
                nc.scalar.copy(y, acc[:])
                if first >= HALF or n == 1:
                    nc.gpsimd.tensor_tensor(dst, y, wgo_sb[:, first : first + count], ALU.mult)
                elif n == PAGES - 1:
                    nc.gpsimd.tensor_tensor(
                        weighted[0][:, 2:],
                        late[:, 1].bitcast(F32),
                        wgo_sb[:, :HALF].unsqueeze(1).to_broadcast([P, 2, HALF]),
                        ALU.mult,
                    )

        def put(n, first, count):
            nc.vector.tensor_copy(
                page[n][:].indirect(place[:, first // LIST : (first + count) // LIST]),
                weighted[first // HALF][:, n, first % HALF : first % HALF + count],
            )

        last = PAGES - 1
        cation(0, 0, "main")
        cation(1, 0, "side")
        quantise_wb(0, 0)
        quantise_wb(1, 0)
        anion(0, 0, "main")
        quantise_wb(0, 1)
        quantise_wb(1, 1)
        anion(1, 0, "main")
        cation(0, 1, "main")
        anion(0, 1, "main")
        cation(1, 1, "main", range(2))
        features(0, 0)
        features(1, 0)
        for b in range(PASSES):
            for u in range(HALF // PIECE):
                cols = slice(u * PIECE, (u + 1) * PIECE)
                h_piece[b, u] = (h_codes[b, 0][:, cols], h_plane[b, 0][:, cols])
        late = keep.tile([P, PASSES, 2, HALF * 2], BF16, name="late", tag="h_last", align_bytes=64)
        weigh(0, 0, PIECE, True)
        weigh(0, PIECE, PIECE, True)
        for n in range(1, PAGES):
            weigh(n, 0, HALF, False)
        put(0, 0, PIECE)
        put(0, PIECE, PIECE)
        for n in range(1, PAGES):
            put(n, 0, HALF)
        cation(1, 1, "side", range(2, PACK))
        anion(1, 1, "side")
        late_features()
        quantise_late(3, late[:, 1])
        h_third = sign_late()
        weigh(0, HALF + PIECE, PIECE, True)
        quantise_late(2, h_third[:])
        weigh(1, HALF + PIECE, PIECE, False)
        for n in range(2):
            weigh(n, HALF, PIECE, False)
        for n in range(2, PAGES):
            weigh(n, HALF, HALF, False)
        for first in (HALF + PIECE, HALF):
            for n in range(2):
                put(n, first, PIECE)
        for n in range(2, PAGES):
            put(n, HALF, HALF)
        tail_tag = "y%d_%d" % (last, HALF)
        sums = keep.tile([P, last, S], F32, name="sums", tag=tail_tag, align_bytes=64)
        for n in range(last):
            cuts = (0, HALF, HALF + PIECE, S) if n == last - 1 else (0, S)
            for cols in map(slice, cuts, cuts[1:]):
                nc.gpsimd.tensor_tensor(sums[:, n, cols], gap[:, n, cols], page[n][:, cols], ALU.subtract)
                nc.scalar.activation(gap[:, n, cols], sums[:, n, cols], ACT.Abs)
                nc.sync.dma_start(out[n * P : (n + 1) * P, cols], gap[:, n, cols])
        result = keep.tile([P, S], F32, name="result", tag=tail_tag, align_bytes=64)
        for u in range(S // PIECE):
            cols = slice(u * PIECE, (u + 1) * PIECE)
            nc.vector.tensor_tensor(gap[:, last, cols], gap[:, last, cols], page[last][:, cols], ALU.subtract)
            nc.scalar.activation(result[:, cols], gap[:, last, cols], ACT.Abs)
            queue = nc.scalar if u == S // PIECE - 1 else nc.sync
            queue.dma_start(out[last * P : (last + 1) * P, cols], result[:, cols])
